import numpy as np
import ml_dtypes


def mxq(x, axis, fmt="e4m3"):
    dtype, down = {"e4m3": (ml_dtypes.float8_e4m3fn, 7), "e5m2": (ml_dtypes.float8_e5m2, 14)}[fmt]
    v = np.moveaxis(np.asarray(x, np.float32).astype(ml_dtypes.bfloat16).astype(np.float64), axis, -1)
    blocks = v.reshape(v.shape[:-1] + (-1, 32))
    amax = np.abs(blocks).max(-1, keepdims=True)
    byte = np.maximum(np.where(amax > 0, np.frexp(amax)[1] - 1 + 127, 0) - down, 1)
    scale = np.exp2(byte - 127.0)
    codes = (blocks / scale).astype(np.float32).astype(dtype).astype(np.float64)
    return np.moveaxis((codes * scale).reshape(v.shape), -1, axis)


WIDE = False


def mx_kscale(k):
    if not WIDE:
        return np.ones(k)
    levels = np.array([10, -10, 5, -5, 0])
    if k % 512:
        return np.exp2(np.random.permutation(np.resize(levels, k // 32))).repeat(32)
    a = np.empty((k // 512, 16))
    for p in range(k // 512):
        a[p, :8] = np.random.permutation(np.resize(levels, 8))
        for g in range(8):
            far = levels[np.abs(levels - a[p, g]) >= 10]
            a[p, g + 8] = far[np.random.randint(len(far))]
    return np.exp2(a.ravel()).repeat(32)


BF16 = ml_dtypes.bfloat16


def bf(x):
    return np.asarray(x, np.float32).astype(BF16)


def f64(x):
    return np.asarray(x).astype(np.float64)


E2M1 = np.array([0.0, 0.5, 1.0, 1.5, 2.0, 3.0, 4.0, 6.0, -0.0, -0.5, -1.0, -1.5, -2.0, -3.0, -4.0, -6.0])


def pack_weight(w, fmt):
    k, n = w.shape
    w = f64(bf(w)).reshape(k // 32, 32, n)
    amax = np.abs(w).max(1)
    if fmt == "e4m3":
        byte = np.frexp(amax)[1] - 1 + 127 - 7
    else:
        mant, ex = np.frexp(amax / 6.0)
        byte = np.where(mant > 0.5, ex, ex - 1) + 127
    byte = np.clip(np.where(amax > 0, byte, 1), 1, 254)
    scaled = (w * np.exp2(127.0 - byte)[:, None, :]).reshape(k, n).astype(np.float32)
    by_word = np.ascontiguousarray(scaled.reshape(k // 512, 128, 4, n).transpose(0, 1, 3, 2))
    if fmt == "e4m3":
        words = by_word.astype(ml_dtypes.float8_e4m3fn).view(np.uint8)
    else:
        c = by_word.astype(ml_dtypes.float4_e2m1fn).view(np.uint8) & 0xF
        words = c[..., 0::2] | (c[..., 1::2] << 4)
    return np.ascontiguousarray(words), np.ascontiguousarray(byte.astype(np.uint8).reshape(k // 512, 16, n))


def unpack_weight(words, scales, fmt):
    g, p, n, _ = words.shape
    if fmt == "e4m3":
        vals = np.ascontiguousarray(words).view(ml_dtypes.float8_e4m3fn).astype(np.float64)
    else:
        nib = np.empty((g, p, n, 4), np.uint8)
        nib[..., 0::2] = words & 0xF
        nib[..., 1::2] = words >> 4
        vals = E2M1[nib]
    vals = vals * np.repeat(np.exp2(scales.astype(np.float64) - 127.0), 8, axis=1)[..., None]
    return vals.transpose(0, 1, 3, 2).reshape(g * 512, n)
def pack4(w):
    words, scales = pack_weight(w, "e2m1")
    return words.reshape(words.shape[0], 128, -1), scales


def unpack4(words, scales):
    return unpack_weight(words.reshape(words.shape[0], 128, -1, 2), scales, "e2m1")


def planes(Y):
    n, m = Y.shape
    b = f64(bf(Y)).reshape(n // 32, 32, m)
    amax = np.abs(b).max(1)
    byte = np.clip(np.where(amax > 0, np.frexp(amax)[1] - 1 + 127 - 7, 1), 1, 254)
    codes = (b * np.exp2(127.0 - byte)[:, None, :]).reshape(n, m).astype(np.float32).astype(ml_dtypes.float8_e4m3fn).view(np.uint8)
    words = codes.reshape(n // 512, 128, 4, m).transpose(0, 1, 3, 2)
    return np.ascontiguousarray(words), np.ascontiguousarray(byte.astype(np.uint8).reshape(n // 512, 16, m))


P, K, F, V = 1536, 1024, 1024, 512


def setup_inputs():
    rn = np.random.standard_normal
    s1, s2 = mx_kscale(K), mx_kscale(K)
    t1, t2 = mx_kscale(F), mx_kscale(F)
    c1_words, c1_scales = pack4(rn((K, P)) * s1[:, None])
    e1_words, e1_scales = pack4(rn((K, F)) / np.sqrt(K) / s1[:, None])
    c2_words, c2_scales = pack4(rn((K, P)) * s2[:, None])
    e2_words, e2_scales = pack4(rn((K, F)) / np.sqrt(K) / s2[:, None])
    return {
        "c1_words": c1_words, "c1_scales": c1_scales, "e1_words": e1_words, "e1_scales": e1_scales,
        "c2_words": c2_words, "c2_scales": c2_scales, "e2_words": e2_words, "e2_scales": e2_scales,
        "gain1": bf((1 + 0.1 * rn(F)) * t1), "offset1": bf(0.3 * rn(F) * t1),
        "gain2": bf((1 + 0.1 * rn(F)) * t2), "offset2": bf(0.3 * rn(F) * t2),
        "w1": bf(rn((F, V)) / np.sqrt(F) / t1[:, None]),
        "w2": bf(rn((F, V)) / np.sqrt(F) / t2[:, None]),
        "r": bf(0.5 * np.exp(0.8 * rn(V))),
    }

def reference(c1_words, c1_scales, e1_words, e1_scales, c2_words, c2_scales, e2_words, e2_scales,
              gain1, offset1, gain2, offset2, w1, w2, r):
    h1 = (unpack4(c1_words, c1_scales).T @ unpack4(e1_words, e1_scales)) * f64(gain1) + f64(offset1)
    h2 = (unpack4(c2_words, c2_scales).T @ unpack4(e2_words, e2_scales)) * f64(gain2) + f64(offset2)
    u1 = mxq(h1, 1, "e4m3") @ mxq(f64(w1), 0, "e4m3")
    u2 = mxq(h2, 1, "e4m3") @ mxq(f64(w2), 0, "e4m3")
    y = np.square(u1 - u2) * f64(r)
    words, scales = planes(y.T)
    return y, words, scales

@@ -1,0 +1,390 @@
+from contextlib import ExitStack
+
+import concourse.mybir as mybir
+from concourse.masks import make_identity
+
+F32 = mybir.dt.float32
+BF16 = mybir.dt.bfloat16
+I32 = mybir.dt.int32
+U32 = mybir.dt.uint32
+U8 = mybir.dt.uint8
+FP8X4 = mybir.dt.float8_e4m3fn_x4
+FP4X4 = mybir.dt.float4_e2m1fn_x4
+ACT = mybir.ActivationFunctionType
+ALU = mybir.AluOpType
+
+PIX, ATOMS, BANDS, VARS = 1536, 1024, 1024, 512
+P = 128
+CHUNK = 512
+TILE = 128
+GROUPS = [(c, d, g) for c, d in ((0, 0), (1, 0), (0, 1), (1, 1), (2, 0), (2, 1)) for g in range(2)]
+FLOPS = 2 * 2 * PIX * ATOMS * BANDS + 2 * 2 * PIX * BANDS * VARS
+
+
+def tile_two_date_alteration_scores_k5_kernel(
+    tc, c1_words, c1_scales, e1_words, e1_scales, c2_words, c2_scales, e2_words, e2_scales,
+    gain1, offset1, gain2, offset2, w1, w2, r, out_0, out_1, out_2,
+):
+    nc = tc.nc
+    c_words, c_scales = (c1_words, c2_words), (c1_scales, c2_scales)
+    e_words, e_scales = (e1_words, e2_words), (e1_scales, e2_scales)
+    weights = (w1, w2)
+
+    with ExitStack() as ctx:
+        keep = ctx.enter_context(tc.tile_pool(name="keep", bufs=1))
+        work = ctx.enter_context(tc.tile_pool(name="work", bufs=3))
+        psum = ctx.enter_context(tc.psum_pool(name="psum", bufs=1))
+        ctx.enter_context(tc.manual_schedule())
+
+        def kept(name, shape, dtype):
+            return keep.tile(shape, dtype, name=name, align_bytes=64)
+
+        e_raw = [[kept("e_raw%d_%d" % (d, g), [P, 2, BANDS], U8) for g in range(2)] for d in range(2)]
+        es_raw = [kept("es_raw%d" % d, [P, 2, BANDS], U8) for d in range(2)]
+        e_cols = [[kept("e_cols%d_%d" % (d, g), [P, 4, 2, 2 * P], U8) for g in range(2)] for d in range(2)]
+        es_cols = [[kept("es_cols%d_%d" % (d, g), [P, 4, 2, P], U8) for g in range(2)] for d in range(2)]
+        c_first = [kept("c_first%d" % d, [P, 2, 2 * CHUNK], U8) for d in range(2)]
+        c_rest = [kept("c_rest%d" % d, [P, 2, 2 * (PIX - CHUNK)], U8) for d in range(2)]
+        cs = [kept("cs%d" % d, [P, 2, PIX], U8) for d in range(2)]
+        w_raw = [[kept("w_raw%d_%d" % (d, g), [P, 4, VARS], BF16) for g in range(2)] for d in range(2)]
+        w_codes = [[kept("w_codes%d_%d" % (d, g), [P, VARS], U32) for g in range(2)] for d in range(2)]
+        w_scales = [[kept("w_scales%d_%d" % (d, g), [P, VARS], U8) for g in range(2)] for d in range(2)]
+        h_codes = [kept("h_codes%d" % n, [P, CHUNK], U32) for n in range(12)]
+        h_scales = [kept("h_scales%d" % n, [P, CHUNK], U8) for n in range(12)]
+        vec_rows = kept("vec_rows", [P, 2, P], BF16)
+        affine = kept("affine", [P, 2, 16], F32)
+        ident_bf = kept("ident_bf", [P, P], BF16)
+        ident_f32 = kept("ident_f32", [P, P], F32)
+        r_rows = kept("r_rows", [P, VARS], BF16)
+        y_codes = kept("y_codes", [P, PIX], U32)
+        y_scales = kept("y_scales", [P, PIX], U8)
+
+        def load_words(dst, src, lo, hi):
+            nc.sync.dma_start(out=dst[:].bitcast(I32), in_=src.rearrange("g p n -> p g n")[:, :, lo:hi].bitcast(I32))
+
+        def load_scales(dst, src, queues):
+            rows = src.rearrange("g (q r) n -> r q g n", r=4)
+            for k in range(4):
+                queues[k].dma_start(out=dst[k:P:32, :, :].bitcast(I32), in_=rows[k].bitcast(I32))
+
+        def load_vector(j, vec):
+            nc.sync.dma_start(
+                out=vec_rows[4 * j : 4 * j + 4, :, :].rearrange("t g (a e) -> t (g a) e", e=4),
+                in_=vec.rearrange("(ga t e) -> t ga e", t=4, e=4),
+            )
+
+        def load_weight(d, g):
+            rows = weights[d][512 * g : 512 * (g + 1), :].rearrange("(a t e) v -> e a t v", t=4, e=4)
+            for e in range(4):
+                nc.sync.dma_start(out=w_raw[d][g][e:P:4, :, :], in_=rows[e])
+
+        def clear_scales(d):
+            nc.vector.memset(es_raw[d][:].bitcast(I32), 0)
+            nc.vector.memset(cs[d][:].bitcast(I32), 0)
+
+        def order_words(d, g):
+            src = e_raw[d][g][:].rearrange("p k n -> p (k n)").bitcast(I32).rearrange("p (ka t w) -> p t ka w", t=4, w=2)
+            dst = e_cols[d][g][:].rearrange("p t k n -> p (t k n)").bitcast(I32).rearrange("p (t ka w) -> p t ka w", t=4, w=2)
+            nc.vector.tensor_copy(out=dst, in_=src)
+
+        def order_scales(d, g):
+            src = es_raw[d][:, :, 512 * g : 512 * (g + 1)].bitcast(I32).rearrange("p k (a t) -> p k a t", t=4)
+            dst = es_cols[d][g][:].bitcast(I32).rearrange("p t k a -> p k a t")
+            nc.vector.tensor_copy(out=dst, in_=src)
+
+        def bank(shape, dtype):
+            return psum.tile(shape, dtype, name="bank", tag="bank", bufs=8)
+
+        def affine_columns():
+            turned = bank([P, 2, P], BF16)
+            for g in range(2):
+                nc.tensor.transpose(turned[:, g, :], vec_rows[:, g, :], ident_bf[:])
+            nc.scalar.activation(out=affine[:, :, 0:8], in_=turned[:, :, 0:8], func=ACT.Copy)
+            nc.scalar.activation(out=affine[:, :, 8:16], in_=turned[:, :, 8:16], func=ACT.Copy, scale=-1.0)
+
+        clear_scales(0)
+        nc.gpsimd.memset(vec_rows[:], 0.0)
+        make_identity(nc, ident_bf[:])
+        nc.scalar.activation(out=ident_f32[:], in_=ident_bf[:], func=ACT.Square)
+        load_words(e_raw[0][0], e_words[0], 0, BANDS)
+        load_words(c_first[0], c_words[0], 0, 2 * CHUNK)
+        load_scales(es_raw[0], e_scales[0], [nc.sync] * 4)
+        load_scales(cs[0], c_scales[0], [nc.sync, nc.sync, nc.gpsimd, nc.gpsimd])
+        for j, vec in enumerate((gain1, offset1, gain2, offset2)):
+            load_vector(j, vec)
+        load_weight(0, 0)
+        load_words(e_raw[0][1], e_words[0], BANDS, 2 * BANDS)
+        load_words(c_rest[0], c_words[0], 2 * CHUNK, 2 * PIX)
+        load_weight(0, 1)
+        order_words(0, 0)
+        order_scales(0, 0)
+        order_scales(0, 1)
+        clear_scales(1)
+        load_words(e_raw[1][0], e_words[1], 0, BANDS)
+        load_words(c_first[1], c_words[1], 0, 2 * CHUNK)
+        load_scales(es_raw[1], e_scales[1], [nc.sync] * 4)
+        load_scales(cs[1], c_scales[1], [nc.sync] * 4)
+        load_weight(1, 0)
+        load_words(e_raw[1][1], e_words[1], BANDS, 2 * BANDS)
+        load_weight(1, 1)
+        load_words(c_rest[1], c_words[1], 2 * CHUNK, 2 * PIX)
+        nc.sync.dma_start(out=r_rows[:], in_=r.partition_broadcast(P))
+
+        h_rows, words_in = {}, {}
+
+        def decode(n, t):
+            c, d, g = GROUPS[n]
+            acc = bank([P, CHUNK], F32)
+            for a in range(2):
+                if c == 0:
+                    moving = c_first[d][:, a, :]
+                else:
+                    moving = c_rest[d][:, a, 2 * CHUNK * (c - 1) : 2 * CHUNK * c]
+                nc.tensor.matmul_mx(
+                    out=acc[:],
+                    lhsT=e_cols[d][g][:, t, a, :].bitcast(FP4X4),
+                    lhsT_scale=es_cols[d][g][:, t, a, :],
+                    rhs=moving.bitcast(FP4X4),
+                    rhs_scale=cs[d][:, a, CHUNK * c : CHUNK * (c + 1)],
+                    start=(a == 0),
+                    stop=(a == 1),
+                )
+            return acc
+
+        def adjust(n, t, acc):
+            c, d, g = GROUPS[n]
+            if t == 0:
+                h_rows[n] = kept("h_rows%d" % n, [P, 4, CHUNK], BF16)
+            col = 8 * d + t
+            nc.scalar.activation(
+                out=h_rows[n][:, t, :], in_=acc[:], func=ACT.Identity,
+                scale=affine[:, g, col : col + 1], bias=affine[:, g, col + 4 : col + 5],
+            )
+
+        def interleave(key, rows):
+            width = rows.shape[2]
+            words_in[key] = work.tile([P, width, 4], BF16, name="words_in", bufs=4, align_bytes=64)
+            nc.vector.tensor_copy(
+                out=words_in[key][:].rearrange("p (c i) t -> p c t i", i=4),
+                in_=rows.rearrange("p t (c i) -> p c t i", i=4),
+            )
+
+        def quantize(key, codes, scales):
+            nc.vector.quantize_mx(out=codes.bitcast(FP8X4), scales=scales, in_=words_in[key][:].rearrange("p c t -> p (c t)"))
+
+        diff, square, score, score_bf, turned, y_in = {}, {}, {}, {}, {}, {}
+
+        def project(m, passes):
+            c, lo = m // 4, TILE * (m % 4)
+            if passes[0] == 0:
+                diff[m] = bank([P, VARS], F32)
+            for j in passes:
+                n = GROUPS.index((c, j // 2, j % 2))
+                nc.tensor.matmul_mx(
+                    out=diff[m][:],
+                    lhsT=h_codes[n][:, lo : lo + TILE].bitcast(FP8X4),
+                    lhsT_scale=h_scales[n][:, lo : lo + TILE],
+                    rhs=w_codes[j // 2][j % 2][:].bitcast(FP8X4),
+                    rhs_scale=w_scales[j // 2][j % 2][:],
+                    start=(j == 0),
+                    stop=(j == 3),
+                )
+
+        def squared(m):
+            square[m] = work.tile([P, VARS], F32, name="square")
+            nc.scalar.activation(out=square[m][:], in_=diff[m][:], func=ACT.Square)
+
+        def scored(m):
+            score[m] = work.tile([P, VARS], F32, name="score", bufs=4)
+            nc.vector.tensor_tensor(out=score[m][:], in0=square[m][:], in1=r_rows[:], op=ALU.mult)
+            nc.sync.dma_start(out=out_0[TILE * m : TILE * (m + 1), :], in_=score[m][:])
+
+        def rounded(m, on_scalar=False):
+            score_bf[m] = work.tile([P, 2, P, 2], BF16, name="score_bf", bufs=6)
+            src = score[m][:].rearrange("x (p u e) -> x u p e", u=2, e=2)
+            if on_scalar:
+                nc.scalar.copy(out=score_bf[m][:], in_=src)
+            else:
+                nc.vector.tensor_copy(out=score_bf[m][:], in_=src)
+
+        def rounded_product(m):
+            score_bf[m] = work.tile([P, 2, P, 2], BF16, name="score_bf", bufs=6)
+            nc.vector.tensor_tensor(
+                out=score_bf[m][:],
+                in0=square[m][:].rearrange("x (p u e) -> x u p e", u=2, e=2),
+                in1=r_rows[:].rearrange("x (p u e) -> x u p e", u=2, e=2),
+                op=ALU.mult,
+            )
+
+        def turn(ms):
+            turned[ms] = bank([P, len(ms), 2, TILE], F32)
+            for k, m in enumerate(ms):
+                pairs = score_bf[m][:].rearrange("x u p e -> x (u p e)").bitcast(F32)
+                for u in range(2):
+                    nc.tensor.transpose(turned[ms][:, k, u, :], pairs[:, P * u : P * (u + 1)], ident_f32[:])
+
+        def gather(ms):
+            words_in[ms] = work.tile([P, len(ms) * TILE, 4], BF16, name="y_words_in", align_bytes=64)
+            nc.scalar.copy(
+                out=words_in[ms][:].rearrange("p x t -> p (x t)").bitcast(F32).rearrange("p (k x u) -> p k x u", k=len(ms), u=2),
+                in_=turned[ms][:].rearrange("p k u x -> p k x u"),
+            )
+
+        def planes(ms):
+            cols = slice(TILE * ms[0], TILE * (ms[-1] + 1))
+            quantize(ms, y_codes[:, cols], y_scales[:, cols])
+
+        def store_codes(lo, hi):
+            nc.sync.dma_start(
+                out=out_1[0].rearrange("p x t -> p (x t)").bitcast(I32)[:, lo:hi], in_=y_codes[:, lo:hi].bitcast(I32)
+            )
+
+        def store_scales(lo, hi, queues):
+            for q in range(4):
+                queues[q].dma_start(
+                    out=out_2[0, 4 * q : 4 * q + 4, lo:hi].bitcast(I32), in_=y_scales[32 * q : 32 * q + 4, lo:hi].bitcast(I32)
+                )
+
+        def weight_words(d, g):
+            interleave(("w", d, g), w_raw[d][g][:])
+
+        def weight_codes(d, g):
+            quantize(("w", d, g), w_codes[d][g][:], w_scales[d][g][:])
+
+        def stage_one(n):
+            for t in range(4):
+                acc = decode(n, t)
+                if n == 0 and t == 0:
+                    affine_columns()
+                adjust(n, t, acc)
+
+        def band_words(n):
+            interleave(n, h_rows[n][:])
+
+        def band_codes(n):
+            quantize(n, h_codes[n][:], h_scales[n][:])
+
+        def stage_two(m):
+            project(m, [0, 1, 2, 3])
+            squared(m)
+
+        def turn_pairs(*pairs):
+            for ms in pairs:
+                turn(ms)
+            for ms in pairs:
+                gather(ms)
+
+        stage_one(0)
+        weight_words(0, 0)
+        order_words(0, 1)
+        weight_codes(0, 0)
+        stage_one(1)
+        stage_one(2)
+        stage_one(3)
+        weight_words(0, 1)
+        band_words(0)
+        weight_codes(0, 1)
+        order_words(1, 0)
+        order_scales(1, 0)
+        order_scales(1, 1)
+        band_codes(0)
+        band_words(1)
+        order_words(1, 1)
+        stage_one(4)
+        stage_one(5)
+        stage_one(6)
+        stage_one(7)
+        weight_words(1, 0)
+        band_codes(1)
+        weight_words(1, 1)
+        weight_codes(1, 0)
+        band_words(4)
+        weight_codes(1, 1)
+        band_words(5)
+        band_codes(4)
+        band_words(2)
+        band_codes(5)
+        stage_two(0)
+        stage_two(1)
+        stage_one(8)
+        band_words(3)
+        band_codes(2)
+        scored(0)
+        band_codes(3)
+        scored(1)
+        band_words(6)
+        rounded(0)
+        stage_two(2)
+        stage_two(3)
+        band_words(7)
+        band_codes(6)
+        rounded(1)
+        scored(2)
+        band_codes(7)
+        scored(3)
+        rounded(2)
+        stage_one(9)
+        band_words(8)
+        rounded(3)
+        stage_two(4)
+        stage_two(5)
+        turn_pairs((0, 1), (2, 3))
+        stage_one(10)
+        band_words(9)
+        band_codes(8)
+        scored(4)
+        band_codes(9)
+        scored(5)
+        planes((0, 1))
+        rounded(4)
+        planes((2, 3))
+        store_codes(0, 4 * TILE)
+        store_scales(0, 4 * TILE, [nc.sync] * 4)
+        rounded(5)
+        stage_two(6)
+        stage_one(11)
+        band_words(10)
+        scored(6)
+        band_codes(10)
+        rounded(6)
+        stage_two(7)
+        for k in range(5):
+            lo = TILE * k
+            if k < 4:
+                interleave((11, k), h_rows[11][:, :, lo : lo + TILE])
+            if k > 0:
+                quantize((11, k - 1), h_codes[11][:, lo - TILE : lo], h_scales[11][:, lo - TILE : lo])
+            if k == 1:
+                scored(7)
+        rounded(7, True)
+        project(8, [0, 1, 2])
+        project(9, [0, 1, 2])
+        project(8, [3])
+        squared(8)
+        project(9, [3])
+        squared(9)
+        turn_pairs((4, 5), (6, 7))
+        scored(8)
+        scored(9)
+        rounded(8)
+        planes((4, 5))
+        rounded(9)
+        planes((6, 7))
+        store_codes(4 * TILE, 8 * TILE)
+        stage_two(10)
+        stage_two(11)
+        turn_pairs((8, 9))
+        scored(10)
+        rounded(10)
+        turn((10,))
+        rounded_product(11)
+        turn((11,))
+        gather((10,))
+        gather((11,))
+        scored(11)
+        planes((8, 9))
+        planes((10,))
+        store_codes(8 * TILE, 11 * TILE)
+        planes((11,))
+        store_codes(11 * TILE, PIX)
+        store_scales(4 * TILE, PIX, [nc.scalar, nc.sync, nc.scalar, nc.sync])

@@ -51,8 +51,9 @@ def tile_two_date_alteration_scores_k5_kernel(
         w_scales = [[kept("w_scales%d_%d" % (d, g), [P, VARS], U8) for g in range(2)] for d in range(2)]
         h_codes = [kept("h_codes%d" % n, [P, CHUNK], U32) for n in range(12)]
         h_scales = [kept("h_scales%d" % n, [P, CHUNK], U8) for n in range(12)]
-        vec_rows = kept("vec_rows", [P, 2, P], BF16)
-        affine = kept("affine", [P, 2, 16], F32)
+        vec_raw = kept("vec_raw", [8, 512], BF16)
+        vec_rows = kept("vec_rows", [P, 4, P], BF16)
+        affine = kept("affine", [P, 4, 8], F32)
         ident_bf = kept("ident_bf", [P, P], BF16)
         ident_f32 = kept("ident_f32", [P, P], F32)
         r_rows = kept("r_rows", [P, VARS], BF16)
@@ -68,10 +69,7 @@ def tile_two_date_alteration_scores_k5_kernel(
                 queues[k].dma_start(out=dst[k:P:32, :, :].bitcast(I32), in_=rows[k].bitcast(I32))
 
         def load_vector(j, vec):
-            nc.sync.dma_start(
-                out=vec_rows[4 * j : 4 * j + 4, :, :].rearrange("t g (a e) -> t (g a) e", e=4),
-                in_=vec.rearrange("(ga t e) -> t ga e", t=4, e=4),
-            )
+            nc.sync.dma_start(out=vec_raw[2 * j : 2 * j + 2, :], in_=vec.rearrange("(g n) -> g n", g=2))
 
         def load_weight(d, g):
             rows = weights[d][512 * g : 512 * (g + 1), :].rearrange("(a t e) v -> e a t v", t=4, e=4)
@@ -96,11 +94,15 @@ def tile_two_date_alteration_scores_k5_kernel(
             return psum.tile(shape, dtype, name="bank", tag="bank", bufs=8)
 
         def affine_columns():
-            turned = bank([P, 2, P], BF16)
-            for g in range(2):
-                nc.tensor.transpose(turned[:, g, :], vec_rows[:, g, :], ident_bf[:])
-            nc.scalar.activation(out=affine[:, :, 0:8], in_=turned[:, :, 0:8], func=ACT.Copy)
-            nc.scalar.activation(out=affine[:, :, 8:16], in_=turned[:, :, 8:16], func=ACT.Copy, scale=-1.0)
+            nc.vector.tensor_copy(
+                out=vec_rows[0:8, :, :].rearrange("j t (a e) -> j t a e", e=4),
+                in_=vec_raw[:].rearrange("j (a t e) -> j t a e", t=4, e=4),
+            )
+            turned = bank([P, 4, P], BF16)
+            for t in range(4):
+                nc.tensor.transpose(turned[:, t, :], vec_rows[:, t, :], ident_bf[:])
+            nc.scalar.activation(out=affine[:, :, 0:4], in_=turned[:, :, 0:4], func=ACT.Copy)
+            nc.scalar.activation(out=affine[:, :, 4:8], in_=turned[:, :, 4:8], func=ACT.Copy, scale=-1.0)
 
         clear_scales(0)
         nc.gpsimd.memset(vec_rows[:], 0.0)
@@ -108,15 +110,16 @@ def tile_two_date_alteration_scores_k5_kernel(
         nc.scalar.activation(out=ident_f32[:], in_=ident_bf[:], func=ACT.Square)
         load_words(e_raw[0][0], e_words[0], 0, BANDS)
         load_words(c_first[0], c_words[0], 0, 2 * CHUNK)
-        load_scales(es_raw[0], e_scales[0], [nc.sync] * 4)
-        load_scales(cs[0], c_scales[0], [nc.sync, nc.sync, nc.gpsimd, nc.gpsimd])
         for j, vec in enumerate((gain1, offset1, gain2, offset2)):
             load_vector(j, vec)
+        load_scales(es_raw[0], e_scales[0], [nc.sync] * 4)
+        load_scales(cs[0], c_scales[0], [nc.sync] * 4)
         load_weight(0, 0)
         load_words(e_raw[0][1], e_words[0], BANDS, 2 * BANDS)
         load_words(c_rest[0], c_words[0], 2 * CHUNK, 2 * PIX)
         load_weight(0, 1)
         order_words(0, 0)
+        affine_columns()
         order_scales(0, 0)
         order_scales(0, 1)
         clear_scales(1)
@@ -155,10 +158,10 @@ def tile_two_date_alteration_scores_k5_kernel(
             c, d, g = GROUPS[n]
             if t == 0:
                 h_rows[n] = kept("h_rows%d" % n, [P, 4, CHUNK], BF16)
-            col = 8 * d + t
+            col = 4 * d + g
             nc.scalar.activation(
                 out=h_rows[n][:, t, :], in_=acc[:], func=ACT.Identity,
-                scale=affine[:, g, col : col + 1], bias=affine[:, g, col + 4 : col + 5],
+                scale=affine[:, t, col : col + 1], bias=affine[:, t, col + 2 : col + 3],
             )
 
         def interleave(key, rows):
@@ -253,10 +256,7 @@ def tile_two_date_alteration_scores_k5_kernel(
 
         def stage_one(n):
             for t in range(4):
-                acc = decode(n, t)
-                if n == 0 and t == 0:
-                    affine_columns()
-                adjust(n, t, acc)
+                adjust(n, t, decode(n, t))
 
         def band_words(n):
             interleave(n, h_rows[n][:])

@@ -17,7 +17,8 @@ PIX, ATOMS, BANDS, VARS = 1536, 1024, 1024, 512
 P = 128
 CHUNK = 512
 TILE = 128
-GROUPS = [(c, d, g) for c, d in ((0, 0), (1, 0), (0, 1), (1, 1), (2, 0), (2, 1)) for g in range(2)]
+GROUPS = [(c, d, g) for d in range(2) for c in range(3) for g in range(2)]
+SETS = [(0, 1), (2, 3), (4, 5), (6, 7), (8, 9), (10,), (11,)]
 FLOPS = 2 * 2 * PIX * ATOMS * BANDS + 2 * 2 * PIX * BANDS * VARS
 
 
@@ -29,6 +30,7 @@ def tile_two_date_alteration_scores_k5_kernel(
     c_words, c_scales = (c1_words, c2_words), (c1_scales, c2_scales)
     e_words, e_scales = (e1_words, e2_words), (e1_scales, e2_scales)
     weights = (w1, w2)
+    vectors = ((gain1, offset1), (gain2, offset2))
 
     with ExitStack() as ctx:
         keep = ctx.enter_context(tc.tile_pool(name="keep", bufs=1))
@@ -42,18 +44,21 @@ def tile_two_date_alteration_scores_k5_kernel(
         e_raw = [[kept("e_raw%d_%d" % (d, g), [P, 2, BANDS], U8) for g in range(2)] for d in range(2)]
         es_raw = [kept("es_raw%d" % d, [P, 2, BANDS], U8) for d in range(2)]
         e_cols = [[kept("e_cols%d_%d" % (d, g), [P, 4, 2, 2 * P], U8) for g in range(2)] for d in range(2)]
-        es_cols = [[kept("es_cols%d_%d" % (d, g), [P, 4, 2, P], U8) for g in range(2)] for d in range(2)]
+        es_cols = [kept("es_cols%d" % d, [P, 4, 2, 2, P], U8) for d in range(2)]
         c_first = [kept("c_first%d" % d, [P, 2, 2 * CHUNK], U8) for d in range(2)]
         c_rest = [kept("c_rest%d" % d, [P, 2, 2 * (PIX - CHUNK)], U8) for d in range(2)]
         cs = [kept("cs%d" % d, [P, 2, PIX], U8) for d in range(2)]
         w_raw = [[kept("w_raw%d_%d" % (d, g), [P, 4, VARS], BF16) for g in range(2)] for d in range(2)]
         w_codes = [[kept("w_codes%d_%d" % (d, g), [P, VARS], U32) for g in range(2)] for d in range(2)]
         w_scales = [[kept("w_scales%d_%d" % (d, g), [P, VARS], U8) for g in range(2)] for d in range(2)]
-        h_codes = [kept("h_codes%d" % n, [P, CHUNK], U32) for n in range(12)]
-        h_scales = [kept("h_scales%d" % n, [P, CHUNK], U8) for n in range(12)]
-        vec_raw = kept("vec_raw", [8, 512], BF16)
-        vec_rows = kept("vec_rows", [P, 4, P], BF16)
-        affine = kept("affine", [P, 4, 8], F32)
+        h_codes = [kept("h_codes%d" % n, [P, 2, CHUNK], U32) for n in range(6)]
+        h_scales = [kept("h_scales%d" % n, [P, 2, CHUNK], U8) for n in range(6)]
+        vec_raw = [kept("vec_raw%d" % d, [4, 512], BF16) for d in range(2)]
+        vec_rows = [kept("vec_rows%d" % d, [P, 4, P], BF16) for d in range(2)]
+        warm_in = kept("warm_in", [P, 4 * P], BF16)
+        warm_codes = kept("warm_codes", [P, P], U32)
+        warm_scales = kept("warm_scales", [P, P], U8)
+        affine = [kept("affine%d" % d, [P, 4, 4], F32) for d in range(2)]
         ident_bf = kept("ident_bf", [P, P], BF16)
         ident_f32 = kept("ident_f32", [P, P], F32)
         r_rows = kept("r_rows", [P, VARS], BF16)
@@ -68,8 +73,9 @@ def tile_two_date_alteration_scores_k5_kernel(
             for k in range(4):
                 queues[k].dma_start(out=dst[k:P:32, :, :].bitcast(I32), in_=rows[k].bitcast(I32))
 
-        def load_vector(j, vec):
-            nc.sync.dma_start(out=vec_raw[2 * j : 2 * j + 2, :], in_=vec.rearrange("(g n) -> g n", g=2))
+        def load_vectors(d):
+            for j, vec in enumerate(vectors[d]):
+                nc.sync.dma_start(out=vec_raw[d][2 * j : 2 * j + 2, :], in_=vec.rearrange("(g n) -> g n", g=2))
 
         def load_weight(d, g):
             rows = weights[d][512 * g : 512 * (g + 1), :].rearrange("(a t e) v -> e a t v", t=4, e=4)
@@ -85,51 +91,67 @@ def tile_two_date_alteration_scores_k5_kernel(
             dst = e_cols[d][g][:].rearrange("p t k n -> p (t k n)").bitcast(I32).rearrange("p (t ka w) -> p t ka w", t=4, w=2)
             nc.vector.tensor_copy(out=dst, in_=src)
 
-        def order_scales(d, g):
-            src = es_raw[d][:, :, 512 * g : 512 * (g + 1)].bitcast(I32).rearrange("p k (a t) -> p k a t", t=4)
-            dst = es_cols[d][g][:].bitcast(I32).rearrange("p t k a -> p k a t")
+        def order_scales(d):
+            src = es_raw[d][:].bitcast(I32).rearrange("p k (ga t) -> p k ga t", t=4)
+            dst = es_cols[d][:].rearrange("p t k g n -> p t k (g n)").bitcast(I32).rearrange("p t k ga -> p k ga t")
             nc.vector.tensor_copy(out=dst, in_=src)
 
         def bank(shape, dtype):
             return psum.tile(shape, dtype, name="bank", tag="bank", bufs=8)
 
-        def affine_columns():
+        def vector_rows(d):
             nc.vector.tensor_copy(
-                out=vec_rows[0:8, :, :].rearrange("j t (a e) -> j t a e", e=4),
-                in_=vec_raw[:].rearrange("j (a t e) -> j t a e", t=4, e=4),
+                out=vec_rows[d][0:4, :, :].rearrange("j t (a e) -> j t a e", e=4),
+                in_=vec_raw[d][:].rearrange("j (a t e) -> j t a e", t=4, e=4),
             )
+
+        def affine_columns(d):
             turned = bank([P, 4, P], BF16)
             for t in range(4):
-                nc.tensor.transpose(turned[:, t, :], vec_rows[:, t, :], ident_bf[:])
-            nc.scalar.activation(out=affine[:, :, 0:4], in_=turned[:, :, 0:4], func=ACT.Copy)
-            nc.scalar.activation(out=affine[:, :, 4:8], in_=turned[:, :, 4:8], func=ACT.Copy, scale=-1.0)
+                nc.tensor.transpose(turned[:, t, :], vec_rows[d][:, t, :], ident_bf[:])
+            nc.scalar.activation(out=affine[d][:], in_=turned[:, :, 0:4], func=ACT.Copy, scale=(1.0, -1.0)[d])
+
+        def warm_up(count):
+            scratch = bank([P, P], F32)
+            for i in range(count):
+                nc.tensor.matmul_mx(
+                    out=scratch[:], lhsT=warm_codes[:].bitcast(FP8X4), lhsT_scale=warm_scales[:],
+                    rhs=warm_codes[:].bitcast(FP8X4), rhs_scale=warm_scales[:], start=True, stop=True,
+                )
+
+        def load_first(d):
+            load_words(e_raw[d][0], e_words[d], 0, BANDS)
+            load_words(c_first[d], c_words[d], 0, 2 * CHUNK)
 
         clear_scales(0)
-        nc.gpsimd.memset(vec_rows[:], 0.0)
+        nc.vector.memset(warm_in[:], 0.0)
+        nc.vector.quantize_mx(out=warm_codes[:].bitcast(FP8X4), scales=warm_scales[:], in_=warm_in[:])
+        nc.gpsimd.memset(vec_rows[0][:], 0.0)
         make_identity(nc, ident_bf[:])
+        nc.gpsimd.memset(vec_rows[1][:], 0.0)
         nc.scalar.activation(out=ident_f32[:], in_=ident_bf[:], func=ACT.Square)
-        load_words(e_raw[0][0], e_words[0], 0, BANDS)
-        load_words(c_first[0], c_words[0], 0, 2 * CHUNK)
-        for j, vec in enumerate((gain1, offset1, gain2, offset2)):
-            load_vector(j, vec)
+        load_first(0)
+        load_vectors(0)
         load_scales(es_raw[0], e_scales[0], [nc.sync] * 4)
         load_scales(cs[0], c_scales[0], [nc.sync] * 4)
         load_weight(0, 0)
         load_words(e_raw[0][1], e_words[0], BANDS, 2 * BANDS)
         load_words(c_rest[0], c_words[0], 2 * CHUNK, 2 * PIX)
         load_weight(0, 1)
+        load_vectors(1)
         order_words(0, 0)
-        affine_columns()
-        order_scales(0, 0)
-        order_scales(0, 1)
+        vector_rows(0)
+        warm_up(8)
+        affine_columns(0)
+        warm_up(4)
+        order_scales(0)
         clear_scales(1)
-        load_words(e_raw[1][0], e_words[1], 0, BANDS)
-        load_words(c_first[1], c_words[1], 0, 2 * CHUNK)
+        load_weight(1, 0)
+        load_weight(1, 1)
         load_scales(es_raw[1], e_scales[1], [nc.sync] * 4)
         load_scales(cs[1], c_scales[1], [nc.sync] * 4)
-        load_weight(1, 0)
+        load_first(1)
         load_words(e_raw[1][1], e_words[1], BANDS, 2 * BANDS)
-        load_weight(1, 1)
         load_words(c_rest[1], c_words[1], 2 * CHUNK, 2 * PIX)
         nc.sync.dma_start(out=r_rows[:], in_=r.partition_broadcast(P))
 
@@ -146,7 +168,7 @@ def tile_two_date_alteration_scores_k5_kernel(
                 nc.tensor.matmul_mx(
                     out=acc[:],
                     lhsT=e_cols[d][g][:, t, a, :].bitcast(FP4X4),
-                    lhsT_scale=es_cols[d][g][:, t, a, :],
+                    lhsT_scale=es_cols[d][:, t, a, g, :],
                     rhs=moving.bitcast(FP4X4),
                     rhs_scale=cs[d][:, a, CHUNK * c : CHUNK * (c + 1)],
                     start=(a == 0),
@@ -156,18 +178,18 @@ def tile_two_date_alteration_scores_k5_kernel(
 
         def adjust(n, t, acc):
             c, d, g = GROUPS[n]
-            if t == 0:
-                h_rows[n] = kept("h_rows%d" % n, [P, 4, CHUNK], BF16)
-            col = 4 * d + g
+            if t == 0 and g == 0:
+                h_rows[n // 2] = work.tile([P, 4, 2, CHUNK], BF16, name="h_rows", bufs=4)
             nc.scalar.activation(
-                out=h_rows[n][:, t, :], in_=acc[:], func=ACT.Identity,
-                scale=affine[:, t, col : col + 1], bias=affine[:, t, col + 2 : col + 3],
+                out=h_rows[n // 2][:, t, g, :], in_=acc[:], func=ACT.Identity,
+                scale=affine[d][:, t, g : g + 1], bias=affine[d][:, t, g + 2 : g + 3],
             )
 
-        def interleave(key, rows):
+        def interleave(key, rows, on_scalar=False):
             width = rows.shape[2]
-            words_in[key] = work.tile([P, width, 4], BF16, name="words_in", bufs=4, align_bytes=64)
-            nc.vector.tensor_copy(
+            words_in[key] = work.tile([P, width, 4], BF16, name="words_in", bufs=3, align_bytes=64)
+            copy = nc.scalar.copy if on_scalar else nc.vector.tensor_copy
+            copy(
                 out=words_in[key][:].rearrange("p (c i) t -> p c t i", i=4),
                 in_=rows.rearrange("p t (c i) -> p c t i", i=4),
             )
@@ -185,8 +207,8 @@ def tile_two_date_alteration_scores_k5_kernel(
                 n = GROUPS.index((c, j // 2, j % 2))
                 nc.tensor.matmul_mx(
                     out=diff[m][:],
-                    lhsT=h_codes[n][:, lo : lo + TILE].bitcast(FP8X4),
-                    lhsT_scale=h_scales[n][:, lo : lo + TILE],
+                    lhsT=h_codes[n // 2][:, n % 2, lo : lo + TILE].bitcast(FP8X4),
+                    lhsT_scale=h_scales[n // 2][:, n % 2, lo : lo + TILE],
                     rhs=w_codes[j // 2][j % 2][:].bitcast(FP8X4),
                     rhs_scale=w_scales[j // 2][j % 2][:],
                     start=(j == 0),
@@ -194,41 +216,47 @@ def tile_two_date_alteration_scores_k5_kernel(
                 )
 
         def squared(m):
-            square[m] = work.tile([P, VARS], F32, name="square")
-            nc.scalar.activation(out=square[m][:], in_=diff[m][:], func=ACT.Square)
+            ms = [s for s in SETS if m in s][0]
+            if m == ms[0]:
+                square[ms] = work.tile([P, len(ms), VARS], F32, name="square", bufs=4)
+            nc.scalar.activation(out=square[ms][:, m - ms[0], :], in_=diff[m][:], func=ACT.Square)
 
-        def scored(m):
-            score[m] = work.tile([P, VARS], F32, name="score", bufs=4)
-            nc.vector.tensor_tensor(out=score[m][:], in0=square[m][:], in1=r_rows[:], op=ALU.mult)
-            nc.sync.dma_start(out=out_0[TILE * m : TILE * (m + 1), :], in_=score[m][:])
-
-        def rounded(m, on_scalar=False):
-            score_bf[m] = work.tile([P, 2, P, 2], BF16, name="score_bf", bufs=6)
-            src = score[m][:].rearrange("x (p u e) -> x u p e", u=2, e=2)
-            if on_scalar:
-                nc.scalar.copy(out=score_bf[m][:], in_=src)
-            else:
-                nc.vector.tensor_copy(out=score_bf[m][:], in_=src)
-
-        def rounded_product(m):
-            score_bf[m] = work.tile([P, 2, P, 2], BF16, name="score_bf", bufs=6)
+        def scored(ms):
+            score[ms] = work.tile([P, len(ms), VARS], F32, name="score", bufs=4)
             nc.vector.tensor_tensor(
-                out=score_bf[m][:],
-                in0=square[m][:].rearrange("x (p u e) -> x u p e", u=2, e=2),
+                out=score[ms][:], in0=square[ms][:], in1=r_rows[:].unsqueeze(1).to_broadcast([P, len(ms), VARS]), op=ALU.mult
+            )
+            rows = out_0[TILE * ms[0] : TILE * (ms[-1] + 1), :]
+            nc.sync.dma_start(out=rows.rearrange("(k x) v -> x k v", x=TILE), in_=score[ms][:])
+
+        def rounded(ms, on_scalar=False):
+            score_bf[ms] = work.tile([P, 2, len(ms) * P, 2], BF16, name="score_bf", bufs=6)
+            src = score[ms][:].rearrange("x k (p u e) -> x u (k p) e", u=2, e=2)
+            if on_scalar:
+                nc.scalar.copy(out=score_bf[ms][:], in_=src)
+            else:
+                nc.vector.tensor_copy(out=score_bf[ms][:], in_=src)
+
+        def rounded_product(ms):
+            score_bf[ms] = work.tile([P, 2, P, 2], BF16, name="score_bf", bufs=6)
+            nc.vector.tensor_tensor(
+                out=score_bf[ms][:],
+                in0=square[ms][:, 0, :].rearrange("x (p u e) -> x u p e", u=2, e=2),
                 in1=r_rows[:].rearrange("x (p u e) -> x u p e", u=2, e=2),
                 op=ALU.mult,
             )
 
         def turn(ms):
             turned[ms] = bank([P, len(ms), 2, TILE], F32)
-            for k, m in enumerate(ms):
-                pairs = score_bf[m][:].rearrange("x u p e -> x (u p e)").bitcast(F32)
+            pairs = score_bf[ms][:].rearrange("x u kp e -> x u (kp e)").bitcast(F32)
+            for k in range(len(ms)):
                 for u in range(2):
-                    nc.tensor.transpose(turned[ms][:, k, u, :], pairs[:, P * u : P * (u + 1)], ident_f32[:])
+                    nc.tensor.transpose(turned[ms][:, k, u, :], pairs[:, u, P * k : P * (k + 1)], ident_f32[:])
 
-        def gather(ms):
-            words_in[ms] = work.tile([P, len(ms) * TILE, 4], BF16, name="y_words_in", align_bytes=64)
-            nc.scalar.copy(
+        def gather(ms, on_scalar=True):
+            words_in[ms] = work.tile([P, len(ms) * TILE, 4], BF16, name="y_words_in", bufs=6, align_bytes=64)
+            copy = nc.scalar.copy if on_scalar else nc.vector.tensor_copy
+            copy(
                 out=words_in[ms][:].rearrange("p x t -> p (x t)").bitcast(F32).rearrange("p (k x u) -> p k x u", k=len(ms), u=2),
                 in_=turned[ms][:].rearrange("p k u x -> p k x u"),
             )
@@ -248,8 +276,8 @@ def tile_two_date_alteration_scores_k5_kernel(
                     out=out_2[0, 4 * q : 4 * q + 4, lo:hi].bitcast(I32), in_=y_scales[32 * q : 32 * q + 4, lo:hi].bitcast(I32)
                 )
 
-        def weight_words(d, g):
-            interleave(("w", d, g), w_raw[d][g][:])
+        def weight_words(d, g, on_scalar=False):
+            interleave(("w", d, g), w_raw[d][g][:], on_scalar)
 
         def weight_codes(d, g):
             quantize(("w", d, g), w_codes[d][g][:], w_scales[d][g][:])
@@ -259,10 +287,10 @@ def tile_two_date_alteration_scores_k5_kernel(
                 adjust(n, t, decode(n, t))
 
         def band_words(n):
-            interleave(n, h_rows[n][:])
+            interleave(n, h_rows[n][:].rearrange("p t g x -> p t (g x)"))
 
         def band_codes(n):
-            quantize(n, h_codes[n][:], h_scales[n][:])
+            quantize(n, h_codes[n][:].rearrange("p g x -> p (g x)"), h_scales[n][:].rearrange("p g x -> p (g x)"))
 
         def stage_two(m):
             project(m, [0, 1, 2, 3])
@@ -275,116 +303,104 @@ def tile_two_date_alteration_scores_k5_kernel(
                 gather(ms)
 
         stage_one(0)
-        weight_words(0, 0)
         order_words(0, 1)
-        weight_codes(0, 0)
+        weight_words(0, 0, False)
         stage_one(1)
+        weight_codes(0, 0)
+        vector_rows(1)
+        weight_words(0, 1, False)
+        weight_words(1, 0, False)
+        weight_words(1, 1, False)
         stage_one(2)
-        stage_one(3)
-        weight_words(0, 1)
-        band_words(0)
+        affine_columns(1)
         weight_codes(0, 1)
+        weight_codes(1, 0)
+        order_scales(1)
+        stage_one(3)
         order_words(1, 0)
-        order_scales(1, 0)
-        order_scales(1, 1)
-        band_codes(0)
-        band_words(1)
-        order_words(1, 1)
         stage_one(4)
         stage_one(5)
-        stage_one(6)
-        stage_one(7)
-        weight_words(1, 0)
-        band_codes(1)
-        weight_words(1, 1)
-        weight_codes(1, 0)
-        band_words(4)
         weight_codes(1, 1)
-        band_words(5)
-        band_codes(4)
-        band_words(2)
-        band_codes(5)
-        stage_two(0)
-        stage_two(1)
+        stage_one(6)
+        band_words(0)
+        order_words(1, 1)
+        band_words(1)
+        stage_one(7)
         stage_one(8)
-        band_words(3)
-        band_codes(2)
-        scored(0)
-        band_codes(3)
-        scored(1)
-        band_words(6)
-        rounded(0)
-        stage_two(2)
-        stage_two(3)
-        band_words(7)
-        band_codes(6)
-        rounded(1)
-        scored(2)
-        band_codes(7)
-        scored(3)
-        rounded(2)
         stage_one(9)
-        band_words(8)
-        rounded(3)
-        stage_two(4)
-        stage_two(5)
-        turn_pairs((0, 1), (2, 3))
+        band_words(2)
+        band_codes(0)
+        band_codes(1)
         stage_one(10)
-        band_words(9)
-        band_codes(8)
-        scored(4)
-        band_codes(9)
-        scored(5)
-        planes((0, 1))
-        rounded(4)
-        planes((2, 3))
-        store_codes(0, 4 * TILE)
-        store_scales(0, 4 * TILE, [nc.sync] * 4)
-        rounded(5)
-        stage_two(6)
+        band_words(3)
+        band_codes(3)
+        project(0, [0, 1, 2, 3])
+        project(1, [0, 1, 2, 3])
+        band_codes(2)
+        squared(0)
+        squared(1)
+        band_words(4)
         stage_one(11)
-        band_words(10)
-        scored(6)
-        band_codes(10)
-        rounded(6)
-        stage_two(7)
-        for k in range(5):
-            lo = TILE * k
-            if k < 4:
-                interleave((11, k), h_rows[11][:, :, lo : lo + TILE])
-            if k > 0:
-                quantize((11, k - 1), h_codes[11][:, lo - TILE : lo], h_scales[11][:, lo - TILE : lo])
-            if k == 1:
-                scored(7)
-        rounded(7, True)
-        project(8, [0, 1, 2])
-        project(9, [0, 1, 2])
-        project(8, [3])
+        project(2, [0, 1, 2, 3])
+        project(3, [0, 1, 2, 3])
+        scored((0, 1))
+        band_codes(4)
+        squared(2)
+        project(4, [0, 1, 2, 3])
+        rounded((0, 1), True)
+        project(5, [0, 1, 2, 3])
+        project(6, [0, 1, 2, 3])
+        squared(3)
+        squared(4)
+        band_words(5)
+        scored((2, 3))
+        turn((0, 1))
+        project(7, [0, 1, 2, 3])
+        squared(5)
+        band_codes(5)
+        project(8, [0, 1, 2, 3])
+        squared(6)
+        rounded((2, 3), True)
+        project(9, [0, 1, 2, 3])
+        project(10, [0, 1, 2, 3])
+        scored((4, 5))
+        project(11, [0, 1, 2, 3])
+        squared(7)
+        gather((0, 1), True)
+        scored((6, 7))
+        rounded((4, 5), False)
         squared(8)
-        project(9, [3])
         squared(9)
-        turn_pairs((4, 5), (6, 7))
-        scored(8)
-        scored(9)
-        rounded(8)
+        rounded((6, 7), True)
+        planes((0, 1))
+        squared(10)
+        scored((8, 9))
+        turn((2, 3))
+        squared(11)
+        turn((4, 5))
+        scored((10,))
+        turn((6, 7))
+        rounded((8, 9), False)
+        gather((2, 3), True)
+        scored((11,))
+        turn((8, 9))
+        planes((2, 3))
+        rounded((10,), True)
+        gather((4, 5), True)
+        rounded_product((11,))
+        gather((6, 7), True)
         planes((4, 5))
-        rounded(9)
         planes((6, 7))
-        store_codes(4 * TILE, 8 * TILE)
-        stage_two(10)
-        stage_two(11)
-        turn_pairs((8, 9))
-        scored(10)
-        rounded(10)
-        turn((10,))
-        rounded_product(11)
-        turn((11,))
-        gather((10,))
-        gather((11,))
-        scored(11)
+        gather((8, 9), True)
+        store_codes(0, 4 * TILE)
         planes((8, 9))
+        turn((10,))
+        gather((10,), True)
+        store_codes(4 * TILE, 8 * TILE)
         planes((10,))
         store_codes(8 * TILE, 11 * TILE)
+        turn((11,))
+        gather((11,), True)
         planes((11,))
+        store_scales(0, PIX, [nc.scalar, nc.sync, nc.scalar, nc.sync])
         store_codes(11 * TILE, PIX)
-        store_scales(4 * TILE, PIX, [nc.scalar, nc.sync, nc.scalar, nc.sync])

@@ -19,6 +19,7 @@ CHUNK = 512
 TILE = 128
 GROUPS = [(c, d, g) for d in range(2) for c in range(3) for g in range(2)]
 SETS = [(0, 1), (2, 3), (4, 5), (6, 7), (8, 9), (10,), (11,)]
+LOW, HIGH = slice(0, VARS // 2), slice(VARS // 2, VARS)
 FLOPS = 2 * 2 * PIX * ATOMS * BANDS + 2 * 2 * PIX * BANDS * VARS
 
 
@@ -51,14 +52,13 @@ def tile_two_date_alteration_scores_k5_kernel(
         w_raw = [[kept("w_raw%d_%d" % (d, g), [P, 4, VARS], BF16) for g in range(2)] for d in range(2)]
         w_codes = [[kept("w_codes%d_%d" % (d, g), [P, VARS], U32) for g in range(2)] for d in range(2)]
         w_scales = [[kept("w_scales%d_%d" % (d, g), [P, VARS], U8) for g in range(2)] for d in range(2)]
-        h_codes = [kept("h_codes%d" % n, [P, 2, CHUNK], U32) for n in range(6)]
-        h_scales = [kept("h_scales%d" % n, [P, 2, CHUNK], U8) for n in range(6)]
-        vec_raw = [kept("vec_raw%d" % d, [4, 512], BF16) for d in range(2)]
-        vec_rows = [kept("vec_rows%d" % d, [P, 4, P], BF16) for d in range(2)]
+        h_codes = [kept("h_codes%d" % n, [P, CHUNK], U32) for n in range(12)]
+        h_scales = [kept("h_scales%d" % n, [P, CHUNK], U8) for n in range(12)]
+        vec_raw = [kept("vec_raw%d" % d, [P, 2, P], BF16) for d in range(2)]
         warm_in = kept("warm_in", [P, 4 * P], BF16)
         warm_codes = kept("warm_codes", [P, P], U32)
         warm_scales = kept("warm_scales", [P, P], U8)
-        affine = [kept("affine%d" % d, [P, 4, 4], F32) for d in range(2)]
+        affine = [kept("affine%d" % d, [P, 8, 2], F32) for d in range(2)]
         ident_bf = kept("ident_bf", [P, P], BF16)
         ident_f32 = kept("ident_f32", [P, P], F32)
         r_rows = kept("r_rows", [P, VARS], BF16)
@@ -68,14 +68,14 @@ def tile_two_date_alteration_scores_k5_kernel(
         def load_words(dst, src, lo, hi):
             nc.sync.dma_start(out=dst[:].bitcast(I32), in_=src.rearrange("g p n -> p g n")[:, :, lo:hi].bitcast(I32))
 
-        def load_scales(dst, src, queues):
+        def load_scales(dst, src, lo, hi):
             rows = src.rearrange("g (q r) n -> r q g n", r=4)
             for k in range(4):
-                queues[k].dma_start(out=dst[k:P:32, :, :].bitcast(I32), in_=rows[k].bitcast(I32))
+                nc.sync.dma_start(out=dst[k:P:32, :, lo:hi].bitcast(I32), in_=rows[k][:, :, lo:hi].bitcast(I32))
 
         def load_vectors(d):
             for j, vec in enumerate(vectors[d]):
-                nc.sync.dma_start(out=vec_raw[d][2 * j : 2 * j + 2, :], in_=vec.rearrange("(g n) -> g n", g=2))
+                nc.sync.dma_start(out=vec_raw[d][j:P:32, :, :], in_=vec.rearrange("(g q n) -> q g n", g=2, q=4))
 
         def load_weight(d, g):
             rows = weights[d][512 * g : 512 * (g + 1), :].rearrange("(a t e) v -> e a t v", t=4, e=4)
@@ -100,16 +100,19 @@ def tile_two_date_alteration_scores_k5_kernel(
             return psum.tile(shape, dtype, name="bank", tag="bank", bufs=8)
 
         def vector_rows(d):
-            nc.vector.tensor_copy(
-                out=vec_rows[d][0:4, :, :].rearrange("j t (a e) -> j t a e", e=4),
-                in_=vec_raw[d][:].rearrange("j (a t e) -> j t a e", t=4, e=4),
-            )
+            vec_rows[d] = work.tile([P, 4, 16, 4], BF16, name="vec_rows", bufs=2, align_bytes=64)
+            nc.vector.tensor_copy(out=vec_rows[d][:], in_=vec_raw[d][:].rearrange("p g (a t e) -> p t (g a) e", t=4, e=4))
+
+        def vector_columns(d):
+            vec_cols[d] = work.tile([P, 8, 32], BF16, name="vec_cols", bufs=2, align_bytes=64)
+            nc.vector.transpose(vec_cols[d][:].rearrange("p c j -> p (c j)"), vec_rows[d][:].rearrange("p t ga e -> p (t ga e)"))
 
         def affine_columns(d):
-            turned = bank([P, 4, P], BF16)
-            for t in range(4):
-                nc.tensor.transpose(turned[:, t, :], vec_rows[d][:, t, :], ident_bf[:])
-            nc.scalar.activation(out=affine[d][:], in_=turned[:, :, 0:4], func=ACT.Copy, scale=(1.0, -1.0)[d])
+            nc.vector.tensor_scalar(
+                out=affine[d][:], in0=vec_cols[d][:, :, 0:2], scalar1=(1.0, -1.0)[d], scalar2=None, op0=ALU.mult
+            )
+
+        vec_rows, vec_cols = {}, {}
 
         def warm_up(count):
             scratch = bank([P, P], F32)
@@ -126,31 +129,32 @@ def tile_two_date_alteration_scores_k5_kernel(
         clear_scales(0)
         nc.vector.memset(warm_in[:], 0.0)
         nc.vector.quantize_mx(out=warm_codes[:].bitcast(FP8X4), scales=warm_scales[:], in_=warm_in[:])
-        nc.gpsimd.memset(vec_rows[0][:], 0.0)
+        nc.gpsimd.memset(vec_raw[0][:], 0.0)
         make_identity(nc, ident_bf[:])
-        nc.gpsimd.memset(vec_rows[1][:], 0.0)
+        nc.gpsimd.memset(vec_raw[1][:], 0.0)
         nc.scalar.activation(out=ident_f32[:], in_=ident_bf[:], func=ACT.Square)
         load_first(0)
         load_vectors(0)
-        load_scales(es_raw[0], e_scales[0], [nc.sync] * 4)
-        load_scales(cs[0], c_scales[0], [nc.sync] * 4)
-        load_weight(0, 0)
+        load_scales(es_raw[0], e_scales[0], 0, BANDS)
+        load_scales(cs[0], c_scales[0], 0, CHUNK)
         load_words(e_raw[0][1], e_words[0], BANDS, 2 * BANDS)
+        load_weight(0, 0)
+        load_scales(cs[0], c_scales[0], CHUNK, PIX)
         load_words(c_rest[0], c_words[0], 2 * CHUNK, 2 * PIX)
         load_weight(0, 1)
         load_vectors(1)
+        warm_up(14)
         order_words(0, 0)
         vector_rows(0)
-        warm_up(8)
-        affine_columns(0)
-        warm_up(4)
         order_scales(0)
+        vector_columns(0)
         clear_scales(1)
+        affine_columns(0)
         load_weight(1, 0)
-        load_weight(1, 1)
-        load_scales(es_raw[1], e_scales[1], [nc.sync] * 4)
-        load_scales(cs[1], c_scales[1], [nc.sync] * 4)
+        load_scales(es_raw[1], e_scales[1], 0, BANDS)
+        load_scales(cs[1], c_scales[1], 0, PIX)
         load_first(1)
+        load_weight(1, 1)
         load_words(e_raw[1][1], e_words[1], BANDS, 2 * BANDS)
         load_words(c_rest[1], c_words[1], 2 * CHUNK, 2 * PIX)
         nc.sync.dma_start(out=r_rows[:], in_=r.partition_broadcast(P))
@@ -178,16 +182,16 @@ def tile_two_date_alteration_scores_k5_kernel(
 
         def adjust(n, t, acc):
             c, d, g = GROUPS[n]
-            if t == 0 and g == 0:
-                h_rows[n // 2] = work.tile([P, 4, 2, CHUNK], BF16, name="h_rows", bufs=4)
+            if t == 0:
+                h_rows[n] = work.tile([P, 4, CHUNK], BF16, name="h_rows", bufs=8)
             nc.scalar.activation(
-                out=h_rows[n // 2][:, t, g, :], in_=acc[:], func=ACT.Identity,
-                scale=affine[d][:, t, g : g + 1], bias=affine[d][:, t, g + 2 : g + 3],
+                out=h_rows[n][:, t, :], in_=acc[:], func=ACT.Identity,
+                scale=affine[d][:, 2 * t + g, 0:1], bias=affine[d][:, 2 * t + g, 1:2],
             )
 
         def interleave(key, rows, on_scalar=False):
             width = rows.shape[2]
-            words_in[key] = work.tile([P, width, 4], BF16, name="words_in", bufs=3, align_bytes=64)
+            words_in[key] = work.tile([P, width, 4], BF16, name="words_in", bufs=4, align_bytes=64)
             copy = nc.scalar.copy if on_scalar else nc.vector.tensor_copy
             copy(
                 out=words_in[key][:].rearrange("p (c i) t -> p c t i", i=4),
@@ -199,27 +203,26 @@ def tile_two_date_alteration_scores_k5_kernel(
 
         diff, square, score, score_bf, turned, y_in = {}, {}, {}, {}, {}, {}
 
-        def project(m, passes):
+        def project(m, cols=slice(0, VARS)):
             c, lo = m // 4, TILE * (m % 4)
-            if passes[0] == 0:
-                diff[m] = bank([P, VARS], F32)
-            for j in passes:
+            diff[m, cols.start] = bank([P, cols.stop - cols.start], F32)
+            for j in range(4):
                 n = GROUPS.index((c, j // 2, j % 2))
                 nc.tensor.matmul_mx(
-                    out=diff[m][:],
-                    lhsT=h_codes[n // 2][:, n % 2, lo : lo + TILE].bitcast(FP8X4),
-                    lhsT_scale=h_scales[n // 2][:, n % 2, lo : lo + TILE],
-                    rhs=w_codes[j // 2][j % 2][:].bitcast(FP8X4),
-                    rhs_scale=w_scales[j // 2][j % 2][:],
+                    out=diff[m, cols.start][:],
+                    lhsT=h_codes[n][:, lo : lo + TILE].bitcast(FP8X4),
+                    lhsT_scale=h_scales[n][:, lo : lo + TILE],
+                    rhs=w_codes[j // 2][j % 2][:, cols].bitcast(FP8X4),
+                    rhs_scale=w_scales[j // 2][j % 2][:, cols],
                     start=(j == 0),
                     stop=(j == 3),
                 )
 
-        def squared(m):
+        def squared(m, cols=slice(0, VARS)):
             ms = [s for s in SETS if m in s][0]
-            if m == ms[0]:
+            if m == ms[0] and cols.start == 0:
                 square[ms] = work.tile([P, len(ms), VARS], F32, name="square", bufs=4)
-            nc.scalar.activation(out=square[ms][:, m - ms[0], :], in_=diff[m][:], func=ACT.Square)
+            nc.scalar.activation(out=square[ms][:, m - ms[0], cols], in_=diff[m, cols.start][:], func=ACT.Square)
 
         def scored(ms):
             score[ms] = work.tile([P, len(ms), VARS], F32, name="score", bufs=4)
@@ -237,12 +240,13 @@ def tile_two_date_alteration_scores_k5_kernel(
             else:
                 nc.vector.tensor_copy(out=score_bf[ms][:], in_=src)
 
-        def rounded_product(ms):
-            score_bf[ms] = work.tile([P, 2, P, 2], BF16, name="score_bf", bufs=6)
+        def rounded_product(ms, cols):
+            if cols.start == 0:
+                score_bf[ms] = work.tile([P, 2, P, 2], BF16, name="score_bf", bufs=6)
             nc.vector.tensor_tensor(
-                out=score_bf[ms][:],
-                in0=square[ms][:, 0, :].rearrange("x (p u e) -> x u p e", u=2, e=2),
-                in1=r_rows[:].rearrange("x (p u e) -> x u p e", u=2, e=2),
+                out=score_bf[ms][:, :, cols.start // 4 : cols.stop // 4, :],
+                in0=square[ms][:, 0, cols].rearrange("x (p u e) -> x u p e", u=2, e=2),
+                in1=r_rows[:, cols].rearrange("x (p u e) -> x u p e", u=2, e=2),
                 op=ALU.mult,
             )
 
@@ -287,120 +291,126 @@ def tile_two_date_alteration_scores_k5_kernel(
                 adjust(n, t, decode(n, t))
 
         def band_words(n):
-            interleave(n, h_rows[n][:].rearrange("p t g x -> p t (g x)"))
+            interleave(n, h_rows[n][:])
 
         def band_codes(n):
-            quantize(n, h_codes[n][:].rearrange("p g x -> p (g x)"), h_scales[n][:].rearrange("p g x -> p (g x)"))
+            quantize(n, h_codes[n][:], h_scales[n][:])
 
-        def stage_two(m):
-            project(m, [0, 1, 2, 3])
-            squared(m)
-
-        def turn_pairs(*pairs):
-            for ms in pairs:
-                turn(ms)
-            for ms in pairs:
-                gather(ms)
-
-        stage_one(0)
         order_words(0, 1)
         weight_words(0, 0, False)
-        stage_one(1)
-        weight_codes(0, 0)
-        vector_rows(1)
-        weight_words(0, 1, False)
-        weight_words(1, 0, False)
-        weight_words(1, 1, False)
-        stage_one(2)
-        affine_columns(1)
-        weight_codes(0, 1)
-        weight_codes(1, 0)
-        order_scales(1)
-        stage_one(3)
-        order_words(1, 0)
-        stage_one(4)
-        stage_one(5)
-        weight_codes(1, 1)
-        stage_one(6)
+        stage_one(0)
         band_words(0)
-        order_words(1, 1)
-        band_words(1)
-        stage_one(7)
-        stage_one(8)
-        stage_one(9)
-        band_words(2)
+        weight_codes(0, 0)
+        weight_words(0, 1, False)
         band_codes(0)
+        stage_one(1)
+        band_words(1)
+        weight_codes(0, 1)
+        weight_words(1, 0, False)
         band_codes(1)
-        stage_one(10)
-        band_words(3)
-        band_codes(3)
-        project(0, [0, 1, 2, 3])
-        project(1, [0, 1, 2, 3])
+        vector_rows(1)
+        order_words(1, 0)
+        vector_columns(1)
+        order_scales(1)
+        affine_columns(1)
+        order_words(1, 1)
+        stage_one(2)
+        band_words(2)
+        weight_codes(1, 0)
+        weight_words(1, 1, False)
         band_codes(2)
-        squared(0)
-        squared(1)
+        stage_one(3)
+        band_words(3)
+        weight_codes(1, 1)
+        stage_one(4)
         band_words(4)
-        stage_one(11)
-        project(2, [0, 1, 2, 3])
-        project(3, [0, 1, 2, 3])
-        scored((0, 1))
-        band_codes(4)
-        squared(2)
-        project(4, [0, 1, 2, 3])
-        rounded((0, 1), True)
-        project(5, [0, 1, 2, 3])
-        project(6, [0, 1, 2, 3])
-        squared(3)
-        squared(4)
+        band_codes(3)
+        stage_one(5)
         band_words(5)
-        scored((2, 3))
-        turn((0, 1))
-        project(7, [0, 1, 2, 3])
-        squared(5)
+        band_codes(4)
+        stage_one(6)
+        band_words(6)
         band_codes(5)
-        project(8, [0, 1, 2, 3])
-        squared(6)
-        rounded((2, 3), True)
-        project(9, [0, 1, 2, 3])
-        project(10, [0, 1, 2, 3])
+        stage_one(7)
+        band_words(7)
+        band_codes(6)
+        stage_one(8)
+        band_words(8)
+        band_codes(7)
+        stage_one(9)
+        band_words(9)
+        band_codes(8)
+        stage_one(10)
+        stage_one(11)
+        project(0)
+        band_words(10)
+        project(1)
+        band_codes(9)
+        squared(0)
+        project(2)
+        squared(1)
+        squared(2)
+        project(3)
+        project(4)
+        scored((0, 1))
+        band_words(11)
+        project(5)
+        band_codes(10)
+        project(6)
+        project(7)
+        squared(3)
+        scored((2, 3))
+        squared(4)
+        squared(5)
+        band_codes(11)
         scored((4, 5))
-        project(11, [0, 1, 2, 3])
+        rounded((0, 1), True)
+        squared(6)
+        project(8)
+        project(9)
         squared(7)
-        gather((0, 1), True)
+        turn((0, 1))
         scored((6, 7))
-        rounded((4, 5), False)
+        rounded((2, 3), True)
         squared(8)
-        squared(9)
-        rounded((6, 7), True)
-        planes((0, 1))
-        squared(10)
-        scored((8, 9))
         turn((2, 3))
-        squared(11)
-        turn((4, 5))
-        scored((10,))
-        turn((6, 7))
+        squared(9)
+        gather((0, 1), True)
+        project(10)
+        rounded((4, 5), False)
+        scored((8, 9))
+        planes((0, 1))
+        rounded((6, 7), True)
+        project(11, LOW)
         rounded((8, 9), False)
+        squared(10)
+        scored((10,))
+        squared(11, LOW)
+        project(11, HIGH)
+        turn((4, 5))
         gather((2, 3), True)
-        scored((11,))
+        squared(11, HIGH)
+        turn((6, 7))
+        gather((4, 5), True)
+        gather((6, 7), True)
+        rounded_product((11,), LOW)
+        rounded((10,), False)
         turn((8, 9))
         planes((2, 3))
-        rounded((10,), True)
-        gather((4, 5), True)
-        rounded_product((11,))
-        gather((6, 7), True)
-        planes((4, 5))
-        planes((6, 7))
+        turn((10,))
         gather((8, 9), True)
         store_codes(0, 4 * TILE)
-        planes((8, 9))
-        turn((10,))
+        scored((11,))
+        rounded_product((11,), HIGH)
         gather((10,), True)
+        planes((4, 5))
+        planes((6, 7))
         store_codes(4 * TILE, 8 * TILE)
-        planes((10,))
-        store_codes(8 * TILE, 11 * TILE)
+        planes((8, 9))
         turn((11,))
+        planes((10,))
         gather((11,), True)
+        store_codes(8 * TILE, 11 * TILE)
         planes((11,))
-        store_scales(0, PIX, [nc.scalar, nc.sync, nc.scalar, nc.sync])
         store_codes(11 * TILE, PIX)
+        store_scales(0, PIX, [nc.scalar, nc.sync, nc.scalar, nc.sync])

@@ -13,14 +13,21 @@ FP4X4 = mybir.dt.float4_e2m1fn_x4
 ACT = mybir.ActivationFunctionType
 ALU = mybir.AluOpType
 
-PIX, ATOMS, BANDS, VARS = 1536, 1024, 1024, 512
+PIXELS, ATOMS, BANDS, VARIATES = 1536, 1024, 1024, 512
 P = 128
+PASS = 4 * P
 CHUNK = 512
 TILE = 128
-GROUPS = [(c, d, g) for d in range(2) for c in range(3) for g in range(2)]
+PSUM_BANKS = 8
+
+GROUPS = [(c, d, g) for d in range(2) for c in range(PIXELS // CHUNK) for g in range(2)]
+FIRST_SPAN, SECOND_SPAN, THIRD_SPAN = (0, 0, CHUNK), (0, CHUNK, PIXELS), (1, 0, PIXELS)
+SPANS = [FIRST_SPAN, SECOND_SPAN, THIRD_SPAN]
 SETS = [(0, 1), (2, 3), (4, 5), (6, 7), (8, 9), (10,), (11,)]
-LOW, HIGH = slice(0, VARS // 2), slice(VARS // 2, VARS)
-FLOPS = 2 * 2 * PIX * ATOMS * BANDS + 2 * 2 * PIX * BANDS * VARS
+WHOLE, LOW, HIGH = slice(0, VARIATES), slice(0, VARIATES // 2), slice(VARIATES // 2, VARIATES)
+WARM_UP_PASSES = 16
+
+FLOPS = 2 * 2 * PIXELS * ATOMS * BANDS + 2 * 2 * PIXELS * BANDS * VARIATES
 
 
 def tile_two_date_alteration_scores_k5_kernel(
@@ -32,320 +39,283 @@ def tile_two_date_alteration_scores_k5_kernel(
     e_words, e_scales = (e1_words, e2_words), (e1_scales, e2_scales)
     weights = (w1, w2)
     vectors = ((gain1, offset1), (gain2, offset2))
+    signs = (1.0, -1.0)
 
     with ExitStack() as ctx:
         keep = ctx.enter_context(tc.tile_pool(name="keep", bufs=1))
-        work = ctx.enter_context(tc.tile_pool(name="work", bufs=3))
-        psum = ctx.enter_context(tc.psum_pool(name="psum", bufs=1))
+        work = ctx.enter_context(tc.tile_pool(name="work", bufs=4))
+        psum = ctx.enter_context(tc.psum_pool(name="psum", bufs=PSUM_BANKS))
         ctx.enter_context(tc.manual_schedule())
 
         def kept(name, shape, dtype):
             return keep.tile(shape, dtype, name=name, align_bytes=64)
 
-        e_raw = [[kept("e_raw%d_%d" % (d, g), [P, 2, BANDS], U8) for g in range(2)] for d in range(2)]
-        es_raw = [kept("es_raw%d" % d, [P, 2, BANDS], U8) for d in range(2)]
+        def bank(shape):
+            return psum.tile(shape, F32, name="bank")
+
+        e_raw = [[kept("e_raw%d_%d" % (d, g), [P, 2, 2 * PASS], U8) for g in range(2)] for d in range(2)]
+        e_scale_raw = [kept("e_scale_raw%d" % d, [P, 2, BANDS], U8) for d in range(2)]
         e_cols = [[kept("e_cols%d_%d" % (d, g), [P, 4, 2, 2 * P], U8) for g in range(2)] for d in range(2)]
-        es_cols = [kept("es_cols%d" % d, [P, 4, 2, 2, P], U8) for d in range(2)]
-        c_first = [kept("c_first%d" % d, [P, 2, 2 * CHUNK], U8) for d in range(2)]
-        c_rest = [kept("c_rest%d" % d, [P, 2, 2 * (PIX - CHUNK)], U8) for d in range(2)]
-        cs = [kept("cs%d" % d, [P, 2, PIX], U8) for d in range(2)]
-        w_raw = [[kept("w_raw%d_%d" % (d, g), [P, 4, VARS], BF16) for g in range(2)] for d in range(2)]
-        w_codes = [[kept("w_codes%d_%d" % (d, g), [P, VARS], U32) for g in range(2)] for d in range(2)]
-        w_scales = [[kept("w_scales%d_%d" % (d, g), [P, VARS], U8) for g in range(2)] for d in range(2)]
-        h_codes = [kept("h_codes%d" % n, [P, CHUNK], U32) for n in range(12)]
-        h_scales = [kept("h_scales%d" % n, [P, CHUNK], U8) for n in range(12)]
+        e_scale_cols = [[kept("e_scale_cols%d_%d" % (d, g), [P, 4, 2, P], U8) for g in range(2)] for d in range(2)]
+        c_cols = {span: kept("c_cols%d_%d" % span[:2], [P, 2, 2 * (span[2] - span[1])], U8) for span in SPANS}
+        c_scale_cols = {span: kept("c_scale_cols%d_%d" % span[:2], [P, 2, span[2] - span[1]], U8) for span in SPANS}
+        w_raw = [[kept("w_raw%d_%d" % (d, g), [P, 4, VARIATES], BF16) for g in range(2)] for d in range(2)]
+        w_codes = [[kept("w_codes%d_%d" % (d, g), [P, VARIATES], U32) for g in range(2)] for d in range(2)]
+        w_scales = [[kept("w_scales%d_%d" % (d, g), [P, VARIATES], U8) for g in range(2)] for d in range(2)]
+        h_codes = [kept("h_codes%d" % n, [P, CHUNK], U32) for n in range(len(GROUPS))]
+        h_scales = [kept("h_scales%d" % n, [P, CHUNK], U8) for n in range(len(GROUPS))]
         vec_raw = [kept("vec_raw%d" % d, [P, 2, P], BF16) for d in range(2)]
+        vec_rows = [kept("vec_rows%d" % d, [P, 4, 16, 4], BF16) for d in range(2)]
+        vec_cols = [kept("vec_cols%d" % d, [P, 8, 32], BF16) for d in range(2)]
+        affine = [kept("affine%d" % d, [P, 8, 2], F32) for d in range(2)]
         warm_in = kept("warm_in", [P, 4 * P], BF16)
         warm_codes = kept("warm_codes", [P, P], U32)
         warm_scales = kept("warm_scales", [P, P], U8)
-        affine = [kept("affine%d" % d, [P, 8, 2], F32) for d in range(2)]
         ident_bf = kept("ident_bf", [P, P], BF16)
         ident_f32 = kept("ident_f32", [P, P], F32)
-        r_rows = kept("r_rows", [P, VARS], BF16)
-        y_codes = kept("y_codes", [P, PIX], U32)
-        y_scales = kept("y_scales", [P, PIX], U8)
+        y_codes = kept("y_codes", [P, PIXELS], U32)
+        y_scales = kept("y_scales", [P, PIXELS], U8)
+        h_rows, words_in, factor = {}, {}, {}
+        diff, square, score, score_bf, turned, y_words_in = {}, {}, {}, {}, {}, {}
 
         def load_words(dst, src, lo, hi):
-            nc.sync.dma_start(out=dst[:].bitcast(I32), in_=src.rearrange("g p n -> p g n")[:, :, lo:hi].bitcast(I32))
+            nc.sync.dma_start(out=dst[:].bitcast(I32), in_=src.rearrange("k p n -> p k n")[:, :, lo:hi].bitcast(I32))
 
         def load_scales(dst, src, lo, hi):
-            rows = src.rearrange("g (q r) n -> r q g n", r=4)
-            for k in range(4):
-                nc.sync.dma_start(out=dst[k:P:32, :, lo:hi].bitcast(I32), in_=rows[k][:, :, lo:hi].bitcast(I32))
+            rows = src.rearrange("k (q j) n -> j q k n", j=4)
+            for j in range(4):
+                nc.sync.dma_start(out=dst[j:P:32, :, :].bitcast(I32), in_=rows[j][:, :, lo:hi].bitcast(I32))
+
+        def load_bands(d, g):
+            load_words(e_raw[d][g], e_words[d], 2 * PASS * g, 2 * PASS * (g + 1))
+
+        def load_band_scales(d):
+            load_scales(e_scale_raw[d], e_scales[d], 0, BANDS)
+
+        def load_pixels(span):
+            load_words(c_cols[span], c_words[span[0]], 2 * span[1], 2 * span[2])
+
+        def load_pixel_scales(span):
+            load_scales(c_scale_cols[span], c_scales[span[0]], span[1], span[2])
 
         def load_vectors(d):
             for j, vec in enumerate(vectors[d]):
                 nc.sync.dma_start(out=vec_raw[d][j:P:32, :, :], in_=vec.rearrange("(g q n) -> q g n", g=2, q=4))
 
         def load_weight(d, g):
-            rows = weights[d][512 * g : 512 * (g + 1), :].rearrange("(a t e) v -> e a t v", t=4, e=4)
+            rows = weights[d][PASS * g : PASS * (g + 1), :].rearrange("(a t e) v -> e a t v", t=4, e=4)
             for e in range(4):
                 nc.sync.dma_start(out=w_raw[d][g][e:P:4, :, :], in_=rows[e])
 
-        def clear_scales(d):
-            nc.vector.memset(es_raw[d][:].bitcast(I32), 0)
-            nc.vector.memset(cs[d][:].bitcast(I32), 0)
+        def load_factor():
+            factor["rows"] = keep.tile([P, VARIATES], BF16, name="r_rows", tag="w_raw1_1", align_bytes=64)
+            nc.sync.dma_start(out=factor["rows"][:], in_=r.partition_broadcast(P))
+
+        def clear(scale_tile):
+            nc.vector.memset(scale_tile[:].bitcast(I32), 0)
 
         def order_words(d, g):
             src = e_raw[d][g][:].rearrange("p k n -> p (k n)").bitcast(I32).rearrange("p (ka t w) -> p t ka w", t=4, w=2)
             dst = e_cols[d][g][:].rearrange("p t k n -> p (t k n)").bitcast(I32).rearrange("p (t ka w) -> p t ka w", t=4, w=2)
             nc.vector.tensor_copy(out=dst, in_=src)
 
-        def order_scales(d):
-            src = es_raw[d][:].bitcast(I32).rearrange("p k (ga t) -> p k ga t", t=4)
-            dst = es_cols[d][:].rearrange("p t k g n -> p t k (g n)").bitcast(I32).rearrange("p t k ga -> p k ga t")
+        def order_scales(d, g, partitions):
+            src = e_scale_raw[d][partitions, :, PASS * g : PASS * (g + 1)].bitcast(I32).rearrange("p k (a t) -> p k a t", t=4)
+            dst = e_scale_cols[d][g][partitions, :, :, :].bitcast(I32).rearrange("p t k a -> p k a t")
             nc.vector.tensor_copy(out=dst, in_=src)
 
-        def bank(shape, dtype):
-            return psum.tile(shape, dtype, name="bank", tag="bank", bufs=8)
-
         def vector_rows(d):
-            vec_rows[d] = work.tile([P, 4, 16, 4], BF16, name="vec_rows", bufs=2, align_bytes=64)
             nc.vector.tensor_copy(out=vec_rows[d][:], in_=vec_raw[d][:].rearrange("p g (a t e) -> p t (g a) e", t=4, e=4))
 
         def vector_columns(d):
-            vec_cols[d] = work.tile([P, 8, 32], BF16, name="vec_cols", bufs=2, align_bytes=64)
             nc.vector.transpose(vec_cols[d][:].rearrange("p c j -> p (c j)"), vec_rows[d][:].rearrange("p t ga e -> p (t ga e)"))
 
         def affine_columns(d):
-            nc.vector.tensor_scalar(
-                out=affine[d][:], in0=vec_cols[d][:, :, 0:2], scalar1=(1.0, -1.0)[d], scalar2=None, op0=ALU.mult
-            )
+            nc.vector.tensor_scalar(out=affine[d][:], in0=vec_cols[d][:, :, 0:2], scalar1=signs[d], scalar2=None, op0=ALU.mult)
 
-        vec_rows, vec_cols = {}, {}
-
-        def warm_up(count):
-            scratch = bank([P, P], F32)
-            for i in range(count):
+        def warm_up():
+            scratch = bank([P, P])
+            for repeat in range(WARM_UP_PASSES):
                 nc.tensor.matmul_mx(
                     out=scratch[:], lhsT=warm_codes[:].bitcast(FP8X4), lhsT_scale=warm_scales[:],
                     rhs=warm_codes[:].bitcast(FP8X4), rhs_scale=warm_scales[:], start=True, stop=True,
                 )
 
-        def load_first(d):
-            load_words(e_raw[d][0], e_words[d], 0, BANDS)
-            load_words(c_first[d], c_words[d], 0, 2 * CHUNK)
+        def quantize(source, code_words, scale_bytes):
+            nc.vector.quantize_mx(out=code_words.bitcast(FP8X4), scales=scale_bytes, in_=source[:].rearrange("p c t -> p (c t)"))
 
-        clear_scales(0)
-        nc.vector.memset(warm_in[:], 0.0)
-        nc.vector.quantize_mx(out=warm_codes[:].bitcast(FP8X4), scales=warm_scales[:], in_=warm_in[:])
-        nc.gpsimd.memset(vec_raw[0][:], 0.0)
-        make_identity(nc, ident_bf[:])
-        nc.gpsimd.memset(vec_raw[1][:], 0.0)
-        nc.scalar.activation(out=ident_f32[:], in_=ident_bf[:], func=ACT.Square)
-        load_first(0)
-        load_vectors(0)
-        load_scales(es_raw[0], e_scales[0], 0, BANDS)
-        load_scales(cs[0], c_scales[0], 0, CHUNK)
-        load_words(e_raw[0][1], e_words[0], BANDS, 2 * BANDS)
-        load_weight(0, 0)
-        load_scales(cs[0], c_scales[0], CHUNK, PIX)
-        load_words(c_rest[0], c_words[0], 2 * CHUNK, 2 * PIX)
-        load_weight(0, 1)
-        load_vectors(1)
-        warm_up(14)
-        order_words(0, 0)
-        vector_rows(0)
-        order_scales(0)
-        vector_columns(0)
-        clear_scales(1)
-        affine_columns(0)
-        load_weight(1, 0)
-        load_scales(es_raw[1], e_scales[1], 0, BANDS)
-        load_scales(cs[1], c_scales[1], 0, PIX)
-        load_first(1)
-        load_weight(1, 1)
-        load_words(e_raw[1][1], e_words[1], BANDS, 2 * BANDS)
-        load_words(c_rest[1], c_words[1], 2 * CHUNK, 2 * PIX)
-        nc.sync.dma_start(out=r_rows[:], in_=r.partition_broadcast(P))
-
-        h_rows, words_in = {}, {}
-
-        def decode(n, t):
-            c, d, g = GROUPS[n]
-            acc = bank([P, CHUNK], F32)
-            for a in range(2):
-                if c == 0:
-                    moving = c_first[d][:, a, :]
-                else:
-                    moving = c_rest[d][:, a, 2 * CHUNK * (c - 1) : 2 * CHUNK * c]
-                nc.tensor.matmul_mx(
-                    out=acc[:],
-                    lhsT=e_cols[d][g][:, t, a, :].bitcast(FP4X4),
-                    lhsT_scale=es_cols[d][:, t, a, g, :],
-                    rhs=moving.bitcast(FP4X4),
-                    rhs_scale=cs[d][:, a, CHUNK * c : CHUNK * (c + 1)],
-                    start=(a == 0),
-                    stop=(a == 1),
-                )
-            return acc
-
-        def adjust(n, t, acc):
-            c, d, g = GROUPS[n]
-            if t == 0:
-                h_rows[n] = work.tile([P, 4, CHUNK], BF16, name="h_rows", bufs=8)
-            nc.scalar.activation(
-                out=h_rows[n][:, t, :], in_=acc[:], func=ACT.Identity,
-                scale=affine[d][:, 2 * t + g, 0:1], bias=affine[d][:, 2 * t + g, 1:2],
+        def words(job):
+            rows = h_rows[job] if job in h_rows else w_raw[job[0]][job[1]]
+            words_in[job] = work.tile([P, CHUNK, 4], BF16, name="words_in", align_bytes=64)
+            nc.vector.tensor_copy(
+                out=words_in[job][:].rearrange("p (c i) t -> p c t i", i=4),
+                in_=rows[:].rearrange("p t (c i) -> p c t i", i=4),
             )
 
-        def interleave(key, rows, on_scalar=False):
-            width = rows.shape[2]
-            words_in[key] = work.tile([P, width, 4], BF16, name="words_in", bufs=4, align_bytes=64)
-            copy = nc.scalar.copy if on_scalar else nc.vector.tensor_copy
-            copy(
-                out=words_in[key][:].rearrange("p (c i) t -> p c t i", i=4),
-                in_=rows.rearrange("p t (c i) -> p c t i", i=4),
-            )
+        def codes(job):
+            if job in h_rows:
+                quantize(words_in[job], h_codes[job][:], h_scales[job][:])
+            else:
+                quantize(words_in[job], w_codes[job[0]][job[1]][:], w_scales[job[0]][job[1]][:])
 
-        def quantize(key, codes, scales):
-            nc.vector.quantize_mx(out=codes.bitcast(FP8X4), scales=scales, in_=words_in[key][:].rearrange("p c t -> p (c t)"))
-
-        diff, square, score, score_bf, turned, y_in = {}, {}, {}, {}, {}, {}
-
-        def project(m, cols=slice(0, VARS)):
-            c, lo = m // 4, TILE * (m % 4)
-            diff[m, cols.start] = bank([P, cols.stop - cols.start], F32)
-            for j in range(4):
-                n = GROUPS.index((c, j // 2, j % 2))
-                nc.tensor.matmul_mx(
-                    out=diff[m, cols.start][:],
-                    lhsT=h_codes[n][:, lo : lo + TILE].bitcast(FP8X4),
-                    lhsT_scale=h_scales[n][:, lo : lo + TILE],
-                    rhs=w_codes[j // 2][j % 2][:, cols].bitcast(FP8X4),
-                    rhs_scale=w_scales[j // 2][j % 2][:, cols],
-                    start=(j == 0),
-                    stop=(j == 3),
+        def stage_one(n):
+            c, d, g = GROUPS[n]
+            span = [s for s in SPANS if s[0] == d and s[1] <= CHUNK * c < s[2]][0]
+            lo = CHUNK * c - span[1]
+            h_rows[n] = work.tile([P, 4, CHUNK], BF16, name="h_rows", bufs=8)
+            for t in range(4):
+                acc = bank([P, CHUNK])
+                for k in range(2):
+                    nc.tensor.matmul_mx(
+                        out=acc[:],
+                        lhsT=e_cols[d][g][:, t, k, :].bitcast(FP4X4),
+                        lhsT_scale=e_scale_cols[d][g][:, t, k, :],
+                        rhs=c_cols[span][:, k, 2 * lo : 2 * (lo + CHUNK)].bitcast(FP4X4),
+                        rhs_scale=c_scale_cols[span][:, k, lo : lo + CHUNK],
+                        start=(k == 0),
+                        stop=(k == 1),
+                    )
+                nc.scalar.activation(
+                    out=h_rows[n][:, t, :], in_=acc[:], func=ACT.Identity,
+                    scale=affine[d][:, 2 * t + g, 0:1], bias=affine[d][:, 2 * t + g, 1:2],
                 )
 
-        def squared(m, cols=slice(0, VARS)):
+        def project(m, cols=WHOLE):
+            c, lo = divmod(TILE * m, CHUNK)
+            diff[m, cols.start] = bank([P, cols.stop - cols.start])
+            for d in range(2):
+                for g in range(2):
+                    n = GROUPS.index((c, d, g))
+                    nc.tensor.matmul_mx(
+                        out=diff[m, cols.start][:],
+                        lhsT=h_codes[n][:, lo : lo + TILE].bitcast(FP8X4),
+                        lhsT_scale=h_scales[n][:, lo : lo + TILE],
+                        rhs=w_codes[d][g][:, cols].bitcast(FP8X4),
+                        rhs_scale=w_scales[d][g][:, cols],
+                        start=(d == 0 and g == 0),
+                        stop=(d == 1 and g == 1),
+                    )
+
+        def squared(m, cols=WHOLE):
             ms = [s for s in SETS if m in s][0]
-            if m == ms[0] and cols.start == 0:
-                square[ms] = work.tile([P, len(ms), VARS], F32, name="square", bufs=4)
+            if ms not in square:
+                square[ms] = work.tile([P, len(ms), VARIATES], F32, name="square")
             nc.scalar.activation(out=square[ms][:, m - ms[0], cols], in_=diff[m, cols.start][:], func=ACT.Square)
 
         def scored(ms):
-            score[ms] = work.tile([P, len(ms), VARS], F32, name="score", bufs=4)
+            score[ms] = work.tile([P, len(ms), VARIATES], F32, name="score")
             nc.vector.tensor_tensor(
-                out=score[ms][:], in0=square[ms][:], in1=r_rows[:].unsqueeze(1).to_broadcast([P, len(ms), VARS]), op=ALU.mult
+                out=score[ms][:], in0=square[ms][:],
+                in1=factor["rows"][:].unsqueeze(1).to_broadcast([P, len(ms), VARIATES]), op=ALU.mult,
             )
             rows = out_0[TILE * ms[0] : TILE * (ms[-1] + 1), :]
-            nc.sync.dma_start(out=rows.rearrange("(k x) v -> x k v", x=TILE), in_=score[ms][:])
+            nc.sync.dma_start(out=rows.rearrange("(m x) v -> x m v", x=TILE), in_=score[ms][:])
 
-        def rounded(ms, on_scalar=False):
+        def pair_tile(ms):
             score_bf[ms] = work.tile([P, 2, len(ms) * P, 2], BF16, name="score_bf", bufs=6)
-            src = score[ms][:].rearrange("x k (p u e) -> x u (k p) e", u=2, e=2)
-            if on_scalar:
-                nc.scalar.copy(out=score_bf[ms][:], in_=src)
-            else:
-                nc.vector.tensor_copy(out=score_bf[ms][:], in_=src)
+
+        def rounded(ms, copy):
+            pair_tile(ms)
+            copy(out=score_bf[ms][:], in_=score[ms][:].rearrange("x m (p u e) -> x u (m p) e", u=2, e=2))
 
         def rounded_product(ms, cols):
-            if cols.start == 0:
-                score_bf[ms] = work.tile([P, 2, P, 2], BF16, name="score_bf", bufs=6)
+            if ms not in score_bf:
+                pair_tile(ms)
             nc.vector.tensor_tensor(
                 out=score_bf[ms][:, :, cols.start // 4 : cols.stop // 4, :],
                 in0=square[ms][:, 0, cols].rearrange("x (p u e) -> x u p e", u=2, e=2),
-                in1=r_rows[:, cols].rearrange("x (p u e) -> x u p e", u=2, e=2),
+                in1=factor["rows"][:, cols].rearrange("x (p u e) -> x u p e", u=2, e=2),
                 op=ALU.mult,
             )
 
         def turn(ms):
-            turned[ms] = bank([P, len(ms), 2, TILE], F32)
-            pairs = score_bf[ms][:].rearrange("x u kp e -> x u (kp e)").bitcast(F32)
-            for k in range(len(ms)):
+            turned[ms] = bank([P, len(ms), 2, TILE])
+            pairs = score_bf[ms][:].rearrange("x u mp e -> x u (mp e)").bitcast(F32)
+            for place in range(len(ms)):
                 for u in range(2):
-                    nc.tensor.transpose(turned[ms][:, k, u, :], pairs[:, u, P * k : P * (k + 1)], ident_f32[:])
+                    nc.tensor.transpose(turned[ms][:, place, u, :], pairs[:, u, P * place : P * (place + 1)], ident_f32[:])
 
-        def gather(ms, on_scalar=True):
-            words_in[ms] = work.tile([P, len(ms) * TILE, 4], BF16, name="y_words_in", bufs=6, align_bytes=64)
-            copy = nc.scalar.copy if on_scalar else nc.vector.tensor_copy
-            copy(
-                out=words_in[ms][:].rearrange("p x t -> p (x t)").bitcast(F32).rearrange("p (k x u) -> p k x u", k=len(ms), u=2),
-                in_=turned[ms][:].rearrange("p k u x -> p k x u"),
+        def gather(ms):
+            y_words_in[ms] = work.tile([P, len(ms) * TILE, 4], BF16, name="y_words_in", bufs=6, align_bytes=64)
+            nc.scalar.copy(
+                out=y_words_in[ms][:].rearrange("p x t -> p (x t)").bitcast(F32).rearrange("p (m x u) -> p m x u", m=len(ms), u=2),
+                in_=turned[ms][:].rearrange("p m u x -> p m x u"),
             )
 
         def planes(ms):
-            cols = slice(TILE * ms[0], TILE * (ms[-1] + 1))
-            quantize(ms, y_codes[:, cols], y_scales[:, cols])
+            pixels = slice(TILE * ms[0], TILE * (ms[-1] + 1))
+            quantize(y_words_in[ms], y_codes[:, pixels], y_scales[:, pixels])
 
-        def store_codes(lo, hi):
-            nc.sync.dma_start(
-                out=out_1[0].rearrange("p x t -> p (x t)").bitcast(I32)[:, lo:hi], in_=y_codes[:, lo:hi].bitcast(I32)
-            )
+        def store_codes(first, last):
+            pixels = slice(TILE * first, TILE * (last + 1))
+            nc.sync.dma_start(out=out_1[0].rearrange("p x t -> p (x t)").bitcast(I32)[:, pixels], in_=y_codes[:, pixels].bitcast(I32))
 
-        def store_scales(lo, hi, queues):
-            for q in range(4):
-                queues[q].dma_start(
-                    out=out_2[0, 4 * q : 4 * q + 4, lo:hi].bitcast(I32), in_=y_scales[32 * q : 32 * q + 4, lo:hi].bitcast(I32)
-                )
+        def store_scales():
+            for q, queue in enumerate((nc.scalar, nc.sync, nc.scalar, nc.sync)):
+                queue.dma_start(out=out_2[0, 4 * q : 4 * q + 4, :].bitcast(I32), in_=y_scales[32 * q : 32 * q + 4, :].bitcast(I32))
 
-        def weight_words(d, g, on_scalar=False):
-            interleave(("w", d, g), w_raw[d][g][:], on_scalar)
-
-        def weight_codes(d, g):
-            quantize(("w", d, g), w_codes[d][g][:], w_scales[d][g][:])
-
-        def stage_one(n):
-            for t in range(4):
-                adjust(n, t, decode(n, t))
-
-        def band_words(n):
-            interleave(n, h_rows[n][:])
-
-        def band_codes(n):
-            quantize(n, h_codes[n][:], h_scales[n][:])
-
+        nc.vector.memset(vec_raw[0][:], 0.0)
+        clear(c_scale_cols[FIRST_SPAN])
+        nc.vector.memset(warm_in[:], 0.0)
+        clear(c_scale_cols[SECOND_SPAN])
+        nc.vector.quantize_mx(out=warm_codes[:].bitcast(FP8X4), scales=warm_scales[:], in_=warm_in[:])
+        nc.vector.memset(vec_raw[1][:], 0.0)
+        clear(e_scale_cols[0][0])
+        clear(e_scale_cols[0][1])
+        clear(e_scale_raw[1])
+        make_identity(nc, ident_bf[:])
+        nc.scalar.activation(out=ident_f32[:], in_=ident_bf[:], func=ACT.Square)
+        load_band_scales(0)
+        load_vectors(0)
+        load_bands(0, 0)
+        load_pixels(FIRST_SPAN)
+        load_pixel_scales(FIRST_SPAN)
+        load_bands(0, 1)
+        load_weight(0, 0)
+        load_pixels(SECOND_SPAN)
+        load_pixel_scales(SECOND_SPAN)
+        load_weight(0, 1)
+        load_vectors(1)
+        warm_up()
+        for q, step in enumerate((vector_rows, vector_columns, affine_columns, lambda d: order_words(d, 0))):
+            order_scales(0, 0, slice(32 * q, 32 * q + 4))
+            step(0)
+        for q in range(4):
+            order_scales(0, 1, slice(32 * q, 32 * q + 4))
+        clear(c_scale_cols[THIRD_SPAN])
+        load_band_scales(1)
+        load_bands(1, 0)
+        load_bands(1, 1)
+        load_weight(1, 0)
+        load_pixel_scales(THIRD_SPAN)
+        load_pixels(THIRD_SPAN)
+        load_weight(1, 1)
         order_words(0, 1)
-        weight_words(0, 0, False)
-        stage_one(0)
-        band_words(0)
-        weight_codes(0, 0)
-        weight_words(0, 1, False)
-        band_codes(0)
-        stage_one(1)
-        band_words(1)
-        weight_codes(0, 1)
-        weight_words(1, 0, False)
-        band_codes(1)
-        vector_rows(1)
-        order_words(1, 0)
-        vector_columns(1)
-        order_scales(1)
-        affine_columns(1)
-        order_words(1, 1)
-        stage_one(2)
-        band_words(2)
-        weight_codes(1, 0)
-        weight_words(1, 1, False)
-        band_codes(2)
-        stage_one(3)
-        band_words(3)
-        weight_codes(1, 1)
-        stage_one(4)
-        band_words(4)
-        band_codes(3)
-        stage_one(5)
-        band_words(5)
-        band_codes(4)
-        stage_one(6)
-        band_words(6)
-        band_codes(5)
-        stage_one(7)
-        band_words(7)
-        band_codes(6)
-        stage_one(8)
-        band_words(8)
-        band_codes(7)
-        stage_one(9)
-        band_words(9)
-        band_codes(8)
+
+        jobs = [(0, 0), 0, 1, (0, 1), 2, (1, 0), 3, (1, 1), 4, 5, 6, 7, 8, 9]
+        for before, job in zip([None] + jobs, jobs):
+            if job == (1, 0):
+                vector_rows(1)
+                order_words(1, 0)
+                vector_columns(1)
+                order_scales(1, 0, slice(0, P))
+                affine_columns(1)
+                order_words(1, 1)
+                order_scales(1, 1, slice(0, P))
+            if isinstance(job, int):
+                stage_one(job)
+            words(job)
+            if job == (1, 1):
+                load_factor()
+            if before is not None:
+                codes(before)
         stage_one(10)
         stage_one(11)
+
         project(0)
-        band_words(10)
+        words(10)
         project(1)
-        band_codes(9)
+        codes(9)
         squared(0)
         project(2)
         squared(1)
@@ -353,64 +323,64 @@ def tile_two_date_alteration_scores_k5_kernel(
         project(3)
         project(4)
         scored((0, 1))
-        band_words(11)
+        words(11)
         project(5)
-        band_codes(10)
+        codes(10)
         project(6)
         project(7)
         squared(3)
         scored((2, 3))
         squared(4)
         squared(5)
-        band_codes(11)
+        codes(11)
         scored((4, 5))
-        rounded((0, 1), True)
+        rounded((0, 1), nc.scalar.copy)
         squared(6)
         project(8)
         project(9)
         squared(7)
         turn((0, 1))
         scored((6, 7))
-        rounded((2, 3), True)
+        rounded((2, 3), nc.scalar.copy)
         squared(8)
         turn((2, 3))
         squared(9)
-        gather((0, 1), True)
+        gather((0, 1))
         project(10)
-        rounded((4, 5), False)
+        rounded((4, 5), nc.vector.tensor_copy)
         scored((8, 9))
         planes((0, 1))
-        rounded((6, 7), True)
+        rounded((6, 7), nc.scalar.copy)
         project(11, LOW)
-        rounded((8, 9), False)
+        rounded((8, 9), nc.vector.tensor_copy)
         squared(10)
         scored((10,))
         squared(11, LOW)
         project(11, HIGH)
         turn((4, 5))
-        gather((2, 3), True)
+        gather((2, 3))
         squared(11, HIGH)
         turn((6, 7))
-        gather((4, 5), True)
-        gather((6, 7), True)
+        gather((4, 5))
+        gather((6, 7))
         rounded_product((11,), LOW)
-        rounded((10,), False)
+        rounded((10,), nc.vector.tensor_copy)
         turn((8, 9))
         planes((2, 3))
         turn((10,))
-        gather((8, 9), True)
-        store_codes(0, 4 * TILE)
+        gather((8, 9))
+        store_codes(0, 3)
         scored((11,))
         rounded_product((11,), HIGH)
-        gather((10,), True)
+        gather((10,))
         planes((4, 5))
         planes((6, 7))
-        store_codes(4 * TILE, 8 * TILE)
+        store_codes(4, 7)
         planes((8, 9))
         turn((11,))
         planes((10,))
-        gather((11,), True)
-        store_codes(8 * TILE, 11 * TILE)
+        gather((11,))
+        store_codes(8, 10)
         planes((11,))
-        store_codes(11 * TILE, PIX)
-        store_scales(0, PIX, [nc.scalar, nc.sync, nc.scalar, nc.sync])
+        store_codes(11, 11)
+        store_scales()

from contextlib import ExitStack

import concourse.mybir as mybir
from concourse.masks import make_identity

F32 = mybir.dt.float32
BF16 = mybir.dt.bfloat16
I32 = mybir.dt.int32
U32 = mybir.dt.uint32
U8 = mybir.dt.uint8
FP8X4 = mybir.dt.float8_e4m3fn_x4
FP4X4 = mybir.dt.float4_e2m1fn_x4
ACT = mybir.ActivationFunctionType
ALU = mybir.AluOpType

PIXELS, ATOMS, BANDS, VARIATES = 1536, 1024, 1024, 512
P = 128
PASS = 4 * P
CHUNK = 512
TILE = 128
PSUM_BANKS = 8

GROUPS = [(c, d, g) for d in range(2) for c in range(PIXELS // CHUNK) for g in range(2)]
FIRST_SPAN, SECOND_SPAN, THIRD_SPAN = (0, 0, CHUNK), (0, CHUNK, PIXELS), (1, 0, PIXELS)
SPANS = [FIRST_SPAN, SECOND_SPAN, THIRD_SPAN]
SETS = [(0, 1), (2, 3), (4, 5), (6, 7), (8, 9), (10,), (11,)]
WHOLE, LOW, HIGH = slice(0, VARIATES), slice(0, VARIATES // 2), slice(VARIATES // 2, VARIATES)
WARM_UP_PASSES = 16

FLOPS = 2 * 2 * PIXELS * ATOMS * BANDS + 2 * 2 * PIXELS * BANDS * VARIATES


def tile_two_date_alteration_scores_k5_kernel(
    tc, c1_words, c1_scales, e1_words, e1_scales, c2_words, c2_scales, e2_words, e2_scales,
    gain1, offset1, gain2, offset2, w1, w2, r, out_0, out_1, out_2,
):
    nc = tc.nc
    c_words, c_scales = (c1_words, c2_words), (c1_scales, c2_scales)
    e_words, e_scales = (e1_words, e2_words), (e1_scales, e2_scales)
    weights = (w1, w2)
    vectors = ((gain1, offset1), (gain2, offset2))
    signs = (1.0, -1.0)

    with ExitStack() as ctx:
        keep = ctx.enter_context(tc.tile_pool(name="keep", bufs=1))
        work = ctx.enter_context(tc.tile_pool(name="work", bufs=4))
        psum = ctx.enter_context(tc.psum_pool(name="psum", bufs=PSUM_BANKS))
        ctx.enter_context(tc.manual_schedule())

        def kept(name, shape, dtype):
            return keep.tile(shape, dtype, name=name, align_bytes=64)

        def bank(shape):
            return psum.tile(shape, F32, name="bank")

        e_raw = [[kept("e_raw%d_%d" % (d, g), [P, 2, 2 * PASS], U8) for g in range(2)] for d in range(2)]
        e_scale_raw = [kept("e_scale_raw%d" % d, [P, 2, BANDS], U8) for d in range(2)]
        e_cols = [[kept("e_cols%d_%d" % (d, g), [P, 4, 2, 2 * P], U8) for g in range(2)] for d in range(2)]
        e_scale_cols = [[kept("e_scale_cols%d_%d" % (d, g), [P, 4, 2, P], U8) for g in range(2)] for d in range(2)]
        c_cols = {span: kept("c_cols%d_%d" % span[:2], [P, 2, 2 * (span[2] - span[1])], U8) for span in SPANS}
        c_scale_cols = {span: kept("c_scale_cols%d_%d" % span[:2], [P, 2, span[2] - span[1]], U8) for span in SPANS}
        w_raw = [[kept("w_raw%d_%d" % (d, g), [P, 4, VARIATES], BF16) for g in range(2)] for d in range(2)]
        w_codes = [[kept("w_codes%d_%d" % (d, g), [P, VARIATES], U32) for g in range(2)] for d in range(2)]
        w_scales = [[kept("w_scales%d_%d" % (d, g), [P, VARIATES], U8) for g in range(2)] for d in range(2)]
        h_codes = [kept("h_codes%d" % n, [P, CHUNK], U32) for n in range(len(GROUPS))]
        h_scales = [kept("h_scales%d" % n, [P, CHUNK], U8) for n in range(len(GROUPS))]
        vec_raw = [kept("vec_raw%d" % d, [P, 2, P], BF16) for d in range(2)]
        vec_rows = [kept("vec_rows%d" % d, [P, 4, 16, 4], BF16) for d in range(2)]
        vec_cols = [kept("vec_cols%d" % d, [P, 8, 32], BF16) for d in range(2)]
        affine = [kept("affine%d" % d, [P, 8, 2], F32) for d in range(2)]
        warm_in = kept("warm_in", [P, 4 * P], BF16)
        warm_codes = kept("warm_codes", [P, P], U32)
        warm_scales = kept("warm_scales", [P, P], U8)
        ident_bf = kept("ident_bf", [P, P], BF16)
        ident_f32 = kept("ident_f32", [P, P], F32)
        y_codes = kept("y_codes", [P, PIXELS], U32)
        y_scales = kept("y_scales", [P, PIXELS], U8)
        h_rows, words_in, factor = {}, {}, {}
        diff, square, score, score_bf, turned, y_words_in = {}, {}, {}, {}, {}, {}

        def load_words(dst, src, lo, hi):
            nc.sync.dma_start(out=dst[:].bitcast(I32), in_=src.rearrange("k p n -> p k n")[:, :, lo:hi].bitcast(I32))

        def load_scales(dst, src, lo, hi):
            rows = src.rearrange("k (q j) n -> j q k n", j=4)
            for j in range(4):
                nc.sync.dma_start(out=dst[j:P:32, :, :].bitcast(I32), in_=rows[j][:, :, lo:hi].bitcast(I32))

        def load_bands(d, g):
            load_words(e_raw[d][g], e_words[d], 2 * PASS * g, 2 * PASS * (g + 1))

        def load_band_scales(d):
            load_scales(e_scale_raw[d], e_scales[d], 0, BANDS)

        def load_pixels(span):
            load_words(c_cols[span], c_words[span[0]], 2 * span[1], 2 * span[2])

        def load_pixel_scales(span):
            load_scales(c_scale_cols[span], c_scales[span[0]], span[1], span[2])

        def load_vectors(d):
            for j, vec in enumerate(vectors[d]):
                nc.sync.dma_start(out=vec_raw[d][j:P:32, :, :], in_=vec.rearrange("(g q n) -> q g n", g=2, q=4))

        def load_weight(d, g):
            rows = weights[d][PASS * g : PASS * (g + 1), :].rearrange("(a t e) v -> e a t v", t=4, e=4)
            for e in range(4):
                nc.sync.dma_start(out=w_raw[d][g][e:P:4, :, :], in_=rows[e])

        def load_factor():
            factor["rows"] = keep.tile([P, VARIATES], BF16, name="r_rows", tag="w_raw1_1", align_bytes=64)
            nc.sync.dma_start(out=factor["rows"][:], in_=r.partition_broadcast(P))

        def clear(scale_tile):
            nc.vector.memset(scale_tile[:].bitcast(I32), 0)

        def order_words(d, g):
            src = e_raw[d][g][:].rearrange("p k n -> p (k n)").bitcast(I32).rearrange("p (ka t w) -> p t ka w", t=4, w=2)
            dst = e_cols[d][g][:].rearrange("p t k n -> p (t k n)").bitcast(I32).rearrange("p (t ka w) -> p t ka w", t=4, w=2)
            nc.vector.tensor_copy(out=dst, in_=src)

        def order_scales(d, g, partitions):
            src = e_scale_raw[d][partitions, :, PASS * g : PASS * (g + 1)].bitcast(I32).rearrange("p k (a t) -> p k a t", t=4)
            dst = e_scale_cols[d][g][partitions, :, :, :].bitcast(I32).rearrange("p t k a -> p k a t")
            nc.vector.tensor_copy(out=dst, in_=src)

        def vector_rows(d):
            nc.vector.tensor_copy(out=vec_rows[d][:], in_=vec_raw[d][:].rearrange("p g (a t e) -> p t (g a) e", t=4, e=4))

        def vector_columns(d):
            nc.vector.transpose(vec_cols[d][:].rearrange("p c j -> p (c j)"), vec_rows[d][:].rearrange("p t ga e -> p (t ga e)"))

        def affine_columns(d):
            nc.vector.tensor_scalar(out=affine[d][:], in0=vec_cols[d][:, :, 0:2], scalar1=signs[d], scalar2=None, op0=ALU.mult)

        def warm_up():
            scratch = bank([P, P])
            for repeat in range(WARM_UP_PASSES):
                nc.tensor.matmul_mx(
                    out=scratch[:], lhsT=warm_codes[:].bitcast(FP8X4), lhsT_scale=warm_scales[:],
                    rhs=warm_codes[:].bitcast(FP8X4), rhs_scale=warm_scales[:], start=True, stop=True,
                )

        def quantize(source, code_words, scale_bytes):
            nc.vector.quantize_mx(out=code_words.bitcast(FP8X4), scales=scale_bytes, in_=source[:].rearrange("p c t -> p (c t)"))

        def words(job):
            rows = h_rows[job] if job in h_rows else w_raw[job[0]][job[1]]
            words_in[job] = work.tile([P, CHUNK, 4], BF16, name="words_in", align_bytes=64)
            nc.vector.tensor_copy(
                out=words_in[job][:].rearrange("p (c i) t -> p c t i", i=4),
                in_=rows[:].rearrange("p t (c i) -> p c t i", i=4),
            )

        def codes(job):
            if job in h_rows:
                quantize(words_in[job], h_codes[job][:], h_scales[job][:])
            else:
                quantize(words_in[job], w_codes[job[0]][job[1]][:], w_scales[job[0]][job[1]][:])

        def stage_one(n):
            c, d, g = GROUPS[n]
            span = [s for s in SPANS if s[0] == d and s[1] <= CHUNK * c < s[2]][0]
            lo = CHUNK * c - span[1]
            h_rows[n] = work.tile([P, 4, CHUNK], BF16, name="h_rows", bufs=8)
            for t in range(4):
                acc = bank([P, CHUNK])
                for k in range(2):
                    nc.tensor.matmul_mx(
                        out=acc[:],
                        lhsT=e_cols[d][g][:, t, k, :].bitcast(FP4X4),
                        lhsT_scale=e_scale_cols[d][g][:, t, k, :],
                        rhs=c_cols[span][:, k, 2 * lo : 2 * (lo + CHUNK)].bitcast(FP4X4),
                        rhs_scale=c_scale_cols[span][:, k, lo : lo + CHUNK],
                        start=(k == 0),
                        stop=(k == 1),
                    )
                nc.scalar.activation(
                    out=h_rows[n][:, t, :], in_=acc[:], func=ACT.Identity,
                    scale=affine[d][:, 2 * t + g, 0:1], bias=affine[d][:, 2 * t + g, 1:2],
                )

        def project(m, cols=WHOLE):
            c, lo = divmod(TILE * m, CHUNK)
            diff[m, cols.start] = bank([P, cols.stop - cols.start])
            for d in range(2):
                for g in range(2):
                    n = GROUPS.index((c, d, g))
                    nc.tensor.matmul_mx(
                        out=diff[m, cols.start][:],
                        lhsT=h_codes[n][:, lo : lo + TILE].bitcast(FP8X4),
                        lhsT_scale=h_scales[n][:, lo : lo + TILE],
                        rhs=w_codes[d][g][:, cols].bitcast(FP8X4),
                        rhs_scale=w_scales[d][g][:, cols],
                        start=(d == 0 and g == 0),
                        stop=(d == 1 and g == 1),
                    )

        def squared(m, cols=WHOLE):
            ms = [s for s in SETS if m in s][0]
            if ms not in square:
                square[ms] = work.tile([P, len(ms), VARIATES], F32, name="square")
            nc.scalar.activation(out=square[ms][:, m - ms[0], cols], in_=diff[m, cols.start][:], func=ACT.Square)

        def scored(ms):
            score[ms] = work.tile([P, len(ms), VARIATES], F32, name="score")
            nc.vector.tensor_tensor(
                out=score[ms][:], in0=square[ms][:],
                in1=factor["rows"][:].unsqueeze(1).to_broadcast([P, len(ms), VARIATES]), op=ALU.mult,
            )
            rows = out_0[TILE * ms[0] : TILE * (ms[-1] + 1), :]
            nc.sync.dma_start(out=rows.rearrange("(m x) v -> x m v", x=TILE), in_=score[ms][:])

        def pair_tile(ms):
            score_bf[ms] = work.tile([P, 2, len(ms) * P, 2], BF16, name="score_bf", bufs=6)

        def rounded(ms, copy):
            pair_tile(ms)
            copy(out=score_bf[ms][:], in_=score[ms][:].rearrange("x m (p u e) -> x u (m p) e", u=2, e=2))

        def rounded_product(ms, cols):
            if ms not in score_bf:
                pair_tile(ms)
            nc.vector.tensor_tensor(
                out=score_bf[ms][:, :, cols.start // 4 : cols.stop // 4, :],
                in0=square[ms][:, 0, cols].rearrange("x (p u e) -> x u p e", u=2, e=2),
                in1=factor["rows"][:, cols].rearrange("x (p u e) -> x u p e", u=2, e=2),
                op=ALU.mult,
            )

        def turn(ms):
            turned[ms] = bank([P, len(ms), 2, TILE])
            pairs = score_bf[ms][:].rearrange("x u mp e -> x u (mp e)").bitcast(F32)
            for place in range(len(ms)):
                for u in range(2):
                    nc.tensor.transpose(turned[ms][:, place, u, :], pairs[:, u, P * place : P * (place + 1)], ident_f32[:])

        def gather(ms):
            y_words_in[ms] = work.tile([P, len(ms) * TILE, 4], BF16, name="y_words_in", bufs=6, align_bytes=64)
            nc.scalar.copy(
                out=y_words_in[ms][:].rearrange("p x t -> p (x t)").bitcast(F32).rearrange("p (m x u) -> p m x u", m=len(ms), u=2),
                in_=turned[ms][:].rearrange("p m u x -> p m x u"),
            )

        def planes(ms):
            pixels = slice(TILE * ms[0], TILE * (ms[-1] + 1))
            quantize(y_words_in[ms], y_codes[:, pixels], y_scales[:, pixels])

        def store_codes(first, last):
            pixels = slice(TILE * first, TILE * (last + 1))
            nc.sync.dma_start(out=out_1[0].rearrange("p x t -> p (x t)").bitcast(I32)[:, pixels], in_=y_codes[:, pixels].bitcast(I32))

        def store_scales():
            for q, queue in enumerate((nc.scalar, nc.sync, nc.scalar, nc.sync)):
                queue.dma_start(out=out_2[0, 4 * q : 4 * q + 4, :].bitcast(I32), in_=y_scales[32 * q : 32 * q + 4, :].bitcast(I32))

        nc.vector.memset(vec_raw[0][:], 0.0)
        clear(c_scale_cols[FIRST_SPAN])
        nc.vector.memset(warm_in[:], 0.0)
        clear(c_scale_cols[SECOND_SPAN])
        nc.vector.quantize_mx(out=warm_codes[:].bitcast(FP8X4), scales=warm_scales[:], in_=warm_in[:])
        nc.vector.memset(vec_raw[1][:], 0.0)
        clear(e_scale_cols[0][0])
        clear(e_scale_cols[0][1])
        clear(e_scale_raw[1])
        make_identity(nc, ident_bf[:])
        nc.scalar.activation(out=ident_f32[:], in_=ident_bf[:], func=ACT.Square)
        load_band_scales(0)
        load_vectors(0)
        load_bands(0, 0)
        load_pixels(FIRST_SPAN)
        load_pixel_scales(FIRST_SPAN)
        load_bands(0, 1)
        load_weight(0, 0)
        load_pixels(SECOND_SPAN)
        load_pixel_scales(SECOND_SPAN)
        load_weight(0, 1)
        load_vectors(1)
        warm_up()
        for q, step in enumerate((vector_rows, vector_columns, affine_columns, lambda d: order_words(d, 0))):
            order_scales(0, 0, slice(32 * q, 32 * q + 4))
            step(0)
        for q in range(4):
            order_scales(0, 1, slice(32 * q, 32 * q + 4))
        clear(c_scale_cols[THIRD_SPAN])
        load_band_scales(1)
        load_bands(1, 0)
        load_bands(1, 1)
        load_weight(1, 0)
        load_pixel_scales(THIRD_SPAN)
        load_pixels(THIRD_SPAN)
        load_weight(1, 1)
        order_words(0, 1)

        jobs = [(0, 0), 0, 1, (0, 1), 2, (1, 0), 3, (1, 1), 4, 5, 6, 7, 8, 9]
        for before, job in zip([None] + jobs, jobs):
            if job == (1, 0):
                vector_rows(1)
                order_words(1, 0)
                vector_columns(1)
                order_scales(1, 0, slice(0, P))
                affine_columns(1)
                order_words(1, 1)
                order_scales(1, 1, slice(0, P))
            if isinstance(job, int):
                stage_one(job)
            words(job)
            if job == (1, 1):
                load_factor()
            if before is not None:
                codes(before)
        stage_one(10)
        stage_one(11)

        project(0)
        words(10)
        project(1)
        codes(9)
        squared(0)
        project(2)
        squared(1)
        squared(2)
        project(3)
        project(4)
        scored((0, 1))
        words(11)
        project(5)
        codes(10)
        project(6)
        project(7)
        squared(3)
        scored((2, 3))
        squared(4)
        squared(5)
        codes(11)
        scored((4, 5))
        rounded((0, 1), nc.scalar.copy)
        squared(6)
        project(8)
        project(9)
        squared(7)
        turn((0, 1))
        scored((6, 7))
        rounded((2, 3), nc.scalar.copy)
        squared(8)
        turn((2, 3))
        squared(9)
        gather((0, 1))
        project(10)
        rounded((4, 5), nc.vector.tensor_copy)
        scored((8, 9))
        planes((0, 1))
        rounded((6, 7), nc.scalar.copy)
        project(11, LOW)
        rounded((8, 9), nc.vector.tensor_copy)
        squared(10)
        scored((10,))
        squared(11, LOW)
        project(11, HIGH)
        turn((4, 5))
        gather((2, 3))
        squared(11, HIGH)
        turn((6, 7))
        gather((4, 5))
        gather((6, 7))
        rounded_product((11,), LOW)
        rounded((10,), nc.vector.tensor_copy)
        turn((8, 9))
        planes((2, 3))
        turn((10,))
        gather((8, 9))
        store_codes(0, 3)
        scored((11,))
        rounded_product((11,), HIGH)
        gather((10,))
        planes((4, 5))
        planes((6, 7))
        store_codes(4, 7)
        planes((8, 9))
        turn((11,))
        planes((10,))
        gather((11,))
        store_codes(8, 10)
        planes((11,))
        store_codes(11, 11)
        store_scales()
